import numpy as np, ml_dtypes
CORES = [16,18,20,22]
N = 4
import mx_ref
BF = ml_dtypes.bfloat16
def gcols(t, e):
    v = np.concatenate([t.reshape(8, 16, -1, 4), np.zeros((8, 16, 1, 4), BF)], axis=2)
    return np.ascontiguousarray(np.stack([v[g][:, e[g]] for g in range(8)])).reshape(128, -1)
def tile(rs):
    return np.stack(rs, axis=2).reshape(128, -1).astype(BF)
def cut(t, i, w=512):
    return t[:, w * i:w * i + w]
def pick(q, e):
    c = np.concatenate([q[0].reshape(128, -1, 4), np.zeros((128, 1, 4), np.uint8)], axis=1); s = np.concatenate([q[1], np.ones((16, 1), np.uint8)], axis=1)
    return (np.ascontiguousarray(c[:, e].reshape(128, -1)), np.ascontiguousarray(s[:, e]))
def join(*qs):
    return (np.concatenate([q[0] for q in qs], axis=1), np.concatenate([q[1] for q in qs], axis=1))
def put(q, e, v):
    c, s = q[0].reshape(128, -1, 4).copy(), q[1].copy(); c[:, e] = v[0].reshape(128, -1, 4); s[:, e] = v[1]
    return (c.reshape(128, -1), s)
def pk(c, s):
    return (np.ascontiguousarray(c), mx_ref.live(s))
def emit(q):
    return q[0], q[1]
def packed(v, rng):
    q = [mx_ref.quantize(np.ascontiguousarray(v[r])) for r in range(N)]
    return np.stack([a for a, b in q]), np.stack([mx_ref.plane(b, rng) for a, b in q])
def values_of_codes():
    e, c = np.zeros((128, 128, 4), np.float32), np.zeros((128, 2, 4), np.uint8)
    e[np.arange(128), np.arange(128), 0] = 1
    c[:127, :, 0] = np.arange(256).reshape(2, 128).T[:127]
    return mx_ref.matmul(mx_ref.quantize(e.reshape(128, 512).astype(BF)), (c.reshape(128, 8), np.full((16, 2), 127, np.uint8))).T.reshape(-1).astype(np.float64)
CODE_VALUE, SCALE_VALUE = values_of_codes(), 2.0 ** (np.arange(256) - 127.0)
def decode(q):
    return (CODE_VALUE[q[0]].reshape(16, 8, -1, 4) * SCALE_VALUE[q[1]][:, None, :, None] + 0.0).reshape(128, -1).astype(np.float32)
def f(rng, *shape):
    return mx_ref.flush((rng.standard_normal(shape, dtype=np.float32) * np.exp2(rng.integers(-2, 3, shape[:-1] + (1,)))).astype(BF))
def wide(rng, *shape, cols=0):
    v = rng.standard_normal(shape, dtype=np.float32) * np.exp2(rng.integers(-12, 13, shape)).astype(np.float32)
    if cols: v *= np.repeat(np.exp2(rng.integers(-cols, cols + 1, shape[:-2] + (1, shape[-1] // 4))) * (rng.random(shape[:-2] + (1, shape[-1] // 4)) > 0.0625), 4, axis=-1).astype(np.float32)
    return mx_ref.flush(v.astype(BF))
C, K, R = 384, 48, 3
def order(p):
    return np.argsort(-(p[::16] + np.float32(0.0)), axis=1, kind="stable")
def numbers_of(rng):
    return {"x": np.array(f(rng, N, 128, 4 * C)), "u": np.array(f(rng, N, 128, 512)), "v": np.array(f(rng, N, 128, 512))}
def weights(rng, w):
    c, p = packed(w, rng)
    return {"wc": c, "ws": p}
def still(rng):
    w = np.zeros((N, 128, 4, 128, 4), np.float32)
    i = np.arange(128)
    for b in range(4): w[:, i, b, i, b] = 32
    return weights(rng, w.reshape(N, 128, 2048).astype(BF))
def signs(rng):
    return np.stack([rng.permutation(8) % 2 * 2.0 - 1.0 for r in range(N)])
def setup_inputs(rng):
    return {**numbers_of(rng), **weights(rng, f(rng, N, 128, 2048))}
def setup_inputs_ties(rng):
    d = numbers_of(rng)
    e = rng.permutation(N)
    x = d["x"].reshape(N, 8, 16, C, 4)
    for r in range(N):
        k = np.zeros(C, int) if r == e[0] else rng.permutation(C) % 3
        a = x[r][:, :8, :3].copy()
        a[:, :, 2] = 0
        x[r][:, :8] = a[:, :, k]
    x[e[1]] = 0
    u = d["u"].reshape(N, 8, 16, 128, 4)
    u[:, :, 8:, ::16] = 0
    w = np.array(f(rng, N, 128, 2048)).reshape(N, 8, 16, 4, 8, 16, 4)
    w[:, :, 8:, :, :, :8] = 0
    return {"x": x.reshape(N, 128, 4 * C), "u": u.reshape(N, 128, 512), "v": d["v"], **weights(rng, w.reshape(N, 128, 2048))}
def setup_inputs_near(rng):
    d = numbers_of(rng)
    x = d["x"].astype(np.float32).reshape(N, 8, 16, C, 4)
    s = np.arange(C) // 2
    g = ((s[:, None] >> np.arange(8)) & 1) * np.exp2(np.arange(8) - 23.0)
    x[:, :, 0] = 0
    x[:, :, 0, :, 0] = signs(rng)[:, :, None]
    x[:, :, 8] = g[:, :4]
    x[:, :, 9] = g[:, 4:]
    x[:, :, 10:] = rng.integers(4, 8, (N, 8, 6, C, 4)) * rng.choice([-1.0, 1.0], (N, 8, 6, C, 4)) * 2.0 ** -20
    u = d["u"].reshape(N, 128, 128, 4)
    k = np.where(rng.permutation(N) < N // 2, 2.0 ** -30, 1.0).astype(np.float32).astype(BF)
    u[:, :, ::16] = 0
    for h in range(0, 128, 16):
        u[:, h, h, 0] = k
        u[:, h + 8:h + 10, h] = k[:, None, None]
    return {"x": x.reshape(N, 128, 4 * C).astype(BF), "u": u.reshape(N, 128, 512), "v": d["v"], **still(rng)}
def setup_inputs_huge(rng):
    d = numbers_of(rng)
    x = 2.0 ** 30 * (0.6 + 0.4 * rng.random((N, 128, C, 4)))
    c = np.stack([rng.permutation(C) % 2 * 2.0 - 1.0 for r in range(N)])
    c[rng.permutation(N) < N // 2] = 1
    x *= c[:, None, :, None]
    u = d["u"].reshape(N, 128, 128, 4)
    a = 2.0 ** 30 * (1 - 0.25 * rng.random((N, 128, 8, 4))) * signs(rng)[:, None, :, None]
    u[:, :, ::16] = a.astype(np.float32).astype(BF)
    return {"x": x.astype(np.float32).reshape(N, 128, 4 * C).astype(BF), "u": u.reshape(N, 128, 512), "v": d["v"], **still(rng)}
def setup_inputs_spread(rng):
    d = setup_inputs(rng)
    d["x"] = wide(rng, N, 128, 4 * C, cols=6)
    return d
def check_inputs(d):
    b = []
    for k in ("x", "u", "v"):
        a = np.abs(d[k].astype(np.float32))
        if not (np.isfinite(a).all() and ((a == 0) | (a >= 2.0 ** -30) & (a <= 2.0 ** 30)).all()): b.append("a value of " + k)
    return b
def reference(x, u, v, wc, ws):
    qu = [mx_ref.quantize(u[r]) for r in range(N)]
    lay = [pk(wc[r], ws[r]) for r in range(N)]
    now = [x[r] for r in range(N)]
    place = np.tile(C + np.arange(K), (8, 1))
    for t in range(R):
        made, o, border = [], [], []
        for r in range(N):
            q = mx_ref.quantize(now[r])
            made.append(tile([mx_ref.matmul(pick(lay[r], np.arange(128 * b, 128 * b + 128)), q) * np.float32(0.03125) for b in range(4)]))
            o.append(order(mx_ref.matmul(qu[r], mx_ref.quantize(made[r]))))
            border.append(mx_ref.quantize(gcols(made[r], o[r][:, :K])))
        came = decode(join(*border)).astype(BF)
        for r in range(N):
            e = np.concatenate([o[r], place], axis=1)
            i = np.argsort(o[r], axis=1)
            now[r] = gcols(np.concatenate([made[r], cut(came, (r + 1) % N, 4 * K)], axis=1), np.take_along_axis(e, i + K, axis=1))
    y, ol = np.zeros((N, 128, C), np.float32), np.zeros((N, 8, C), np.float32)
    oc, osc = np.zeros((N, 128, 4 * C), np.uint8), np.zeros((N, 16, C), np.uint8)
    for r in range(N):
        q = mx_ref.quantize(now[r])
        y[r] = mx_ref.matmul(mx_ref.quantize(v[r]), q)
        ol[r] = o[r]
        oc[r], osc[r] = emit(q)
    return {"y": y, "ol": ol, "oc": oc, "osc": osc}

@@ -1,0 +1,315 @@
+from concourse.mybir import dt, AluOpType as A, ActivationFunctionType as F
+
+C, K, R = 384, 48, 3
+H = C // 2
+NB = C // 16
+MS = 10
+FW = C + 16
+MID = (C + K) // 2
+BIG = 2.0 ** 90
+STEP, TINY = 0.6 * 2.0 ** -23, 2.0 ** -125
+Q4, U8 = "float8_e4m3fn_x4", "uint8"
+
+SCRATCH = {
+    "xin": ("sbuf", [128, 4 * C], "bfloat16"), "uin": ("sbuf", [128, 512], "bfloat16"), "vin": ("sbuf", [128, 512], "bfloat16"),
+    "wq": ("sbuf", [128, 512], Q4), "wp": ("sbuf", [128, 512], U8),
+    "uq": ("sbuf", [128, 128], Q4), "up": ("sbuf", [128, 128], U8),
+    "uq2": ("sbuf", [128, 128], Q4), "up2": ("sbuf", [128, 128], U8),
+    "vq": ("sbuf", [128, 128], Q4), "vp": ("sbuf", [128, 128], U8),
+    "eq": ("sbuf", [128, 512], Q4), "ep": ("sbuf", [128, 512], U8),
+    "et": ("sbuf", [128, 2048], "bfloat16"), "ones": ("sbuf", [128, 128], "bfloat16"), "ident": ("sbuf", [128, 128], "bfloat16"),
+    "pi": ("sbuf", [128, 8], "int32"), "pj": ("sbuf", [128, 8], "int32"), "pf": ("sbuf", [128, 8], "float32"), "pq": ("sbuf", [128, 8], "float32"),
+    "ui": ("sbuf", [128, 8], "int32"), "uoff": ("sbuf", [128, 8], "uint16"),
+    "n16": ("sbuf", [128, C], "float32"), "tmp": ("sbuf", [128, C], "float32"),
+    "cm": ("sbuf", [128, C], "float32"), "cs": ("sbuf", [128, C], "float32"),
+    "mask4": ("sbuf", [128, C], "bfloat16"), "keep4": ("sbuf", [128, C], "bfloat16"), "jj": ("sbuf", [128, C], "bfloat16"),
+    "xg": ("sbuf", [128, 4 * C], "bfloat16"), "dd": ("sbuf", [128, 4 * C], "bfloat16"),
+    "mm": ("sbuf", [128, C], "float32"), "hh": ("sbuf", [128, C], "float32"), "ee": ("sbuf", [128, C], "float32"), "zz": ("sbuf", [128, 2 * C], "float32"),
+    "ff": ("sbuf", [128, NB, FW], "bfloat16"), "so": ("sbuf", [128, (NB - MS) * FW // 2], "bfloat16"), "cnt": ("sbuf", [128, NB], "float32"),
+    "off": ("sbuf", [128, NB], "uint16"), "oo": ("sbuf", [128, C + K], "bfloat16"),
+    "bm": ("sbuf", [128, K], "bfloat16"), "bs": ("sbuf", [128, K], "bfloat16"),
+    "em": ("sbuf", [128, C], "bfloat16"), "es": ("sbuf", [128, C], "bfloat16"), "xoff": ("sbuf", [128, C // 4], "uint16"),
+    "olb": ("sbuf", [128, C], "float32"), "yb": ("sbuf", [128, C], "float32"),
+}
+for _t in range(R + 1):
+    SCRATCH["qx%d" % _t] = ("sbuf", [128, C], Q4)
+    SCRATCH["px%d" % _t] = ("sbuf", [128, C], U8)
+for _t in range(R):
+    SCRATCH["yw%d" % _t] = ("sbuf", [128, 4 * (C + K)], "bfloat16")
+    SCRATCH["qy%d" % _t] = ("sbuf", [128, C], Q4)
+    SCRATCH["py%d" % _t] = ("sbuf", [128, C], U8)
+    SCRATCH["lq%d" % _t] = ("sbuf", [128, C], Q4)
+    SCRATCH["lp%d" % _t] = ("sbuf", [128, C], U8)
+    SCRATCH["lst%d" % _t] = ("sbuf", [128, K // 4], "uint16")
+    SCRATCH["ll%d" % _t] = ("sbuf", [128, K // 4], "uint16")
+for _b in range(8):
+    SCRATCH["ps%d" % _b] = ("psum", [128, 512], "float32")
+
+SEMAPHORES = (["lx0", "lx1", "lwc", "lws", "lu", "lv", "st", "snt",
+               "ones", "ident", "etz", "etc", "qe", "gp", "pi", "pf", "pq", "gn16", "gj", "t16", "cm", "vc0", "vc", "mask4",
+               "uoff", "qu", "upk", "qv",
+               "gA", "gB", "qx0", "qx1", "yA", "yB", "qy0", "qy1", "pv0", "pv1", "pz0", "pz1", "m0", "m1", "e0", "e1", "zh", "h1", "eqf",
+               "cA", "cB", "scn", "sA", "sB", "cnt", "offv", "offs", "sct", "bm", "bs", "lst", "em", "es", "xoff", "dM", "dE", "ext", "olb",
+               "ym0", "ym1", "yb0", "yb1"]
+              + ["r%d" % i for i in range(8)] + ["aq%d" % i for i in range(R)] + ["al%d" % i for i in range(R)])
+
+
+def rank_program(g, core, T, topo):
+    rank = T.rank_of(core)
+    if rank is None:
+        return
+    n = len(T.cores)
+    dst = T.cores[(rank - 1) % n]
+    rid, pid = topo.addr(dst)[0], topo.addr(dst)[1]
+    mask = topo.mask(core, dst)
+    ne = len(topo.engines(core, dst))
+    V, S, P, Y = g.vector, g.scalar, g.tensor, g.sync
+    qn = {"g": g, "v": V, "s": S, "p": P, "y": Y}
+    count, seen = {}, {}
+
+    def sig(ins, name, k=1):
+        ins.then_inc(T.sem[name], k)
+        count[name] = count.get(name, 0) + k
+
+    def wait(q, *names):
+        for name in names:
+            if seen.get((q, name), 0) < count[name]:
+                qn[q].wait_ge(T.sem[name], count[name])
+                seen[(q, name)] = count[name]
+
+    def u8(v):
+        return v.bitcast(dt.uint8)
+
+    ps = [T["ps%d" % b] for b in range(8)]
+
+    sig(Y.dma_start(T.xin[:, 0:4 * H], T.x[:, 0:4 * H]), "lx0", 16)
+    sig(S.dma_start(T.wp[:], T.ws[:]), "lws", 16)
+    sig(Y.dma_start(u8(T.wq[:]), T.wc[:]), "lwc", 16)
+    sig(S.dma_start(T.xin[:, 4 * H:4 * C], T.x[:, 4 * H:4 * C]), "lx1", 16)
+    sig(Y.dma_start(T.uin[:], T.u[:]), "lu", 16)
+
+    sig(V.memset(T.ones[:], 1.0), "ones")
+    sig(V.memset(T.et[:], 0.0), "etz")
+    sig(g.iota(T.pi[:, 0:1], [[1, 1]], 0, 1), "gp")
+    sig(g.iota(T.ui[:], [[16, 8]], 0, 0), "gp")
+    wait("g", "ones")
+    sig(g.affine_select(T.ident[:], T.ones[:], [[-1, 128]], A.is_equal, 0.0, 0, 1), "ident")
+    sig(g.iota(T.n16[:], [[0, NB], [1, 16]], 0, 0, allow_small_or_imprecise_dtypes=True), "gn16")
+    sig(g.iota(T.jj[:], [[1, C]], -MID, 0, allow_small_or_imprecise_dtypes=True), "gj")
+    sig(g.iota(T.oo[:, C:C + K], [[1, K]], C - MID, 0, allow_small_or_imprecise_dtypes=True), "gj")
+    wait("v", "gp")
+    sig(V.tensor_scalar(T.pj[:, 0:1], T.pi[:, 0:1], 15, None, A.bitwise_and), "pi")
+    sig(V.tensor_scalar(T.pj[:, 1:2], T.pi[:, 0:1], 12, None, A.bitwise_and), "pi")
+    sig(V.tensor_scalar(T.pj[:, 2:3], T.pi[:, 0:1], 3, None, A.bitwise_and), "pi")
+    sig(V.tensor_copy(T.uoff[:], T.ui[:]), "uoff")
+    sig(V.memset(T.cs[:], BIG), "vc0")
+    wait("v", "pi")
+    sig(V.tensor_copy(T.pf[:, 0:1], T.pj[:, 0:1]), "pf")
+    sig(V.tensor_scalar(T.pf[:, 1:2], T.pj[:, 1:2], 4.0, None, A.mult), "pf")
+    sig(V.tensor_scalar(T.pf[:, 2:3], T.pj[:, 2:3], float(4 * MID), None, A.add), "pf")
+    sig(V.memset(T.keep4[:], 1.0), "vc0")
+    wait("v", "pf")
+    sig(V.tensor_scalar(T.pq[:, 0:4], T.ui[:, 0:4], T.pf[:, 1:2], None, A.is_equal), "pq")
+    wait("v", "vc0")
+    sig(V.memset(T.cs[:, 0:C:16], -BIG), "vc")
+    sig(V.memset(T.keep4[:, 0:C:4], 0.0), "vc")
+    wait("s", "ident", "etz")
+    for b in range(4):
+        sig(S.activation(T.et[:, 512 * b + b:512 * (b + 1):4], T.ident[:], F.Copy), "etc")
+    wait("v", "etc")
+    sig(V.quantize_mx(T.eq[:], T.ep[:], T.et[:]), "qe")
+    wait("s", "pf", "gn16")
+    sig(S.activation(T.tmp[:], T.n16[:], F.Abs, bias=T.pf[:, 0:1], scale=-1.0), "t16")
+    wait("s", "pq", "ones")
+    for k in range(4):
+        sig(S.activation(T.mask4[:, k:C:4], T.ones[:, 0:C // 4], F.Copy, scale=T.pq[:, k:k + 1]), "mask4")
+    wait("s", "t16")
+    sig(S.activation(T.cm[:], T.tmp[:], F.Identity, bias=BIG / 2, scale=-BIG), "cm")
+    tadd = T.pf[:, 2:3]
+
+    def state(t):
+        qx, px = T["qx%d" % t], T["px%d" % t]
+        src = T.xin if t == 0 else T.xg
+        cuts = [0, 2 * H, 4 * H, 4 * H + 288, 4 * C]
+
+        def pick(i):
+            a, b = cuts[i], cuts[i + 1]
+            w = T["yw%d" % (t - 1)][:].indirect(T.xoff[:, a // 16:b // 16])
+            if i % 2 == 0:
+                sig(V.tensor_copy(T.xg[:, a:b], w), "gA" if i < 2 else "gB")
+            else:
+                sig(S.activation(T.xg[:, a:b], w, F.Copy), "gA" if i < 2 else "gB")
+        if t:
+            wait("v", "xoff", "ext")
+            wait("s", "xoff", "ext")
+            pick(0)
+            pick(1)
+            pick(3)
+        wait("v", "gA" if t else "lx0")
+        sig(V.quantize_mx(qx[:, 0:H], px[:, 0:H], src[:, 0:4 * H]), "qx0")
+        if t:
+            pick(2)
+        wait("v", "gB" if t else "lx1")
+        sig(V.quantize_mx(qx[:, H:C], px[:, H:C], src[:, 4 * H:4 * C]), "qx1")
+
+    for t in range(R):
+        qx, px, qy, py, yw = T["qx%d" % t], T["px%d" % t], T["qy%d" % t], T["py%d" % t], T["yw%d" % t]
+        state(t)
+        wait("p", "lwc", "lws")
+        for h in range(2):
+            wait("p", "qx%d" % h)
+            for b in ((2, 0, 3, 1) if h == 0 else (0, 1, 3, 2)):
+                sig(P.matmul_mx(ps[4 * h + b][:, 0:H], T.wq[:, 128 * b:128 * b + 128], T.wp[:, 128 * b:128 * b + 128],
+                                qx[:, h * H:h * H + H], px[:, h * H:h * H + H], True, True), "r%d" % (4 * h + b))
+        if t == 0:
+            wait("v", "lu", "uoff")
+            sig(V.quantize_mx(T.uq[:], T.up[:], T.uin[:]), "qu")
+
+        def evac(q, h, b):
+            wait(q, "r%d" % (4 * h + b))
+            o, i = yw[:, 4 * H * h + b:4 * H * (h + 1):4], ps[4 * h + b][:, 0:H]
+            ins = V.tensor_scalar(o, i, 0.03125, None, A.mult) if q == "v" else S.activation(o, i, F.Copy, scale=0.03125)
+            sig(ins, "yB" if h else "yA")
+        evac("v", 0, 0)
+        evac("s", 0, 2)
+        evac("v", 0, 1)
+        evac("s", 0, 3)
+        if t == 0:
+            wait("v", "qu")
+            sig(V.tensor_copy(T.uq2[:].bitcast(dt.uint32), T.uq[:].bitcast(dt.uint32).indirect(T.uoff[:])), "upk")
+            sig(V.tensor_copy(T.up2[:], T.up[:].indirect(T.uoff[:])), "upk")
+        wait("v", "yA")
+        sig(V.quantize_mx(qy[:, 0:H], py[:, 0:H], yw[:, 0:4 * H]), "qy0")
+        evac("s", 1, 0)
+        evac("v", 1, 3)
+        evac("s", 1, 1)
+        evac("s", 1, 2)
+        wait("v", "yB")
+        sig(V.quantize_mx(qy[:, H:C], py[:, H:C], yw[:, 4 * H:4 * C]), "qy1")
+        wait("p", "upk")
+        for h in range(2):
+            wait("p", "qy%d" % h)
+            for k in (1, 0):
+                sig(P.matmul_mx(ps[2 * h + k][:, 0:H], T.uq2[:], T.up2[:], qy[:, h * H:h * H + H], py[:, h * H:h * H + H], True, True),
+                    ("pv%d" if k == 0 else "pz%d") % h)
+        wait("g", "qy0", "qy1")
+        g.remote_dma(u8(T["lq%d" % t][:]), u8(qy[:]), T.sem["aq%d" % t], T.sem.snt, pid, rid, mask)
+        g.remote_dma(T["lp%d" % t][:], py[:], T.sem["aq%d" % t], T.sem.snt, pid, rid, mask)
+        count["snt"] = count.get("snt", 0) + 2 * ne
+        count["aq%d" % t] = 2 * ne
+        if t == 0:
+            wait("y", "qy1")
+            sig(Y.dma_start(T.vin[:], T.v[:]), "lv", 16)
+            wait("v", "cm", "vc", "pf", "mask4", "gj")
+        for h in range(2):
+            a, b = h * H, h * H + H
+            wait("s", "pz%d" % h)
+            sig(S.activation(T.ee[:, a:b], ps[2 * h + 1][:, 0:H], F.Abs, bias=TINY, scale=STEP), "e%d" % h)
+            sig(S.activation(T.zz[:, C + a:C + b], ps[2 * h + 1][:, 0:H], F.Copy), "zh")
+
+        def own(h):
+            wait("v", "pv%d" % h)
+            sig(V.tensor_tensor(T.mm[:, h * H:h * H + H], ps[2 * h][:, 0:H], T.cm[:, h * H:h * H + H], A.min), "m%d" % h)
+
+        def lowered(h):
+            wait("v", "pv%d" % h, "e%d" % h)
+            sig(V.tensor_tensor(T.zz[:, h * H:h * H + H], ps[2 * h][:, 0:H], T.ee[:, h * H:h * H + H], A.subtract), "zh")
+
+        def held(h):
+            wait("v", "m%d" % h)
+            sig(V.tensor_tensor_scan(T.hh[:, h * H:h * H + H], T.cs[:, h * H:h * H + H], T.mm[:, h * H:h * H + H], 0.0, A.min, A.max),
+                "h1" if h else "zh")
+        own(0)
+        lowered(0)
+        held(0)
+        lowered(1)
+        own(1)
+        wait("s", "zh")
+        w2 = FW // 2
+        vhalf, shalf = (MS + NB) // 2, MS // 2
+        for m in range(MS):
+            sig(S.activation(T.ff[:, m, 0:C], T.zz[:, 16 * m + 16:16 * m + 16 + C], F.Sign, bias=T.hh[:, 16 * m + 15:16 * m + 16], scale=-1.0),
+                "sA" if m < shalf else "sB")
+        held(1)
+        wait("v", "zh")
+        for m in range(MS, NB):
+            if m == NB // 2:
+                wait("v", "h1")
+                for h in range(2):
+                    sig(V.tensor_tensor(T.ff[:, h * NB // 2:(h + 1) * NB // 2, C:FW], ps[2 * h][:, 0:H], T.hh[:, h * H:h * H + H], A.is_equal), "eqf")
+            sig(V.tensor_scalar(T.ff[:, m, 0:C], T.zz[:, 16 * m + 16:16 * m + 16 + C], T.hh[:, 16 * m + 15:16 * m + 16], 0.5,
+                                A.is_lt, A.subtract), "cA" if m < vhalf else "cB")
+        for m in range(MS, NB):
+            wait("v", "eqf", "cA" if m < vhalf else "cB")
+            k = m - MS
+            sig(V.tensor_tensor_scan(T.so[:, w2 * k:w2 * k + w2], T.ff[:, m, 0:w2], T.ff[:, m, w2:FW], 0.0, A.add, A.add), "scn")
+        for m in range(MS):
+            wait("s", "eqf", "sA" if m < shalf else "sB")
+            sig(S.activation(T.ff[:, m, :], T.ff[:, m, :], F.Relu, accum_out=T.cnt[:, m:m + 1]), "cnt")
+        wait("p", "qe", "aq%d" % t)
+        for b in range(4):
+            sig(P.matmul_mx(ps[4 + b][:, 0:C], T.eq[:, 128 * b:128 * b + 128], T.ep[:, 128 * b:128 * b + 128],
+                            T["lq%d" % t][:], T["lp%d" % t][:], True, True), "dM")
+        wait("s", "dM")
+        for b in range(4):
+            sig(S.activation(T.dd[:, b:4 * C:4], ps[4 + b][:, 0:C], F.Copy), "dE")
+        wait("v", "scn")
+        sig(V.tensor_scalar(T.off[:, MS:NB], T.so[:, w2 - 1:w2 * (NB - MS):w2], -1.0, float(C // 2), A.mult, A.add), "offv")
+        wait("v", "offv")
+        sig(V.tensor_copy(T.oo[:, 0:C].indirect(T.off[:, MS:NB]), T.jj[:, 16 * MS:C]), "sct")
+        wait("v", "cnt")
+        sig(V.tensor_scalar(T.off[:, 0:MS], T.cnt[:, 0:MS], -1.0, float(C), A.mult, A.add), "offs")
+        wait("v", "offs", "sct")
+        sig(V.tensor_copy(T.oo[:, 0:C].indirect(T.off[:, 0:MS]), T.jj[:, 0:16 * MS]), "sct")
+        wait("v", "sct")
+        sig(V.tensor_tensor(T.bm[:], T.oo[:, 0:K], T.mask4[:, 0:K], A.mult), "bm")
+        wait("v", "bm")
+        sig(V.tensor_tensor_scan(T.bs[:], T.keep4[:, 0:K], T.bm[:], 0.0, A.mult, A.add), "bs")
+        wait("v", "bs")
+        sig(V.tensor_scalar(T["lst%d" % t][:], T.bs[:, 3:K:4], 4.0, tadd, A.mult, A.add), "lst")
+        wait("g", "lst")
+        g.remote_dma(T["ll%d" % t][:], T["lst%d" % t][:], T.sem["al%d" % t], T.sem.snt, pid, rid, mask)
+        count["snt"] += ne
+        count["al%d" % t] = ne
+        sig(V.tensor_tensor(T.em[:], T.oo[:, K:C + K].indirect(T.off[:]), T.mask4[:], A.mult), "em")
+        wait("v", "em")
+        sig(V.tensor_tensor_scan(T.es[:], T.keep4[:], T.em[:], 0.0, A.mult, A.add), "es")
+        wait("v", "es")
+        sig(V.tensor_scalar(T.xoff[:], T.es[:, 3:C:4], 4.0, tadd, A.mult, A.add), "xoff")
+        if t == 0:
+            wait("v", "lv")
+            sig(V.quantize_mx(T.vq[:], T.vp[:], T.vin[:]), "qv")
+        if t == R - 1:
+            wait("s", "sct")
+            sig(S.activation(T.olb[:], T.oo[:, 0:C], F.Identity, bias=float(MID)), "olb")
+            wait("y", "olb")
+            sig(Y.dma_start(T.ol[:], T.olb[0:128:16, :]), "st", 16)
+        ll = T["ll%d" % t]
+        wait("v", "dE", "al%d" % t)
+        wait("s", "dE", "al%d" % t)
+        sig(V.tensor_copy(yw[:, 4 * C:4 * C + 2 * K], T.dd[:].indirect(ll[:, 0:K // 8])), "ext")
+        sig(S.activation(yw[:, 4 * C + 2 * K:4 * C + 4 * K], T.dd[:].indirect(ll[:, K // 8:K // 4]), F.Copy), "ext")
+
+    state(R)
+    qx, px = T["qx%d" % R], T["px%d" % R]
+    wait("p", "qv")
+    for h in range(2):
+        wait("p", "qx%d" % h)
+        sig(P.matmul_mx(ps[h][:, 0:H], T.vq[:], T.vp[:], qx[:, h * H:h * H + H], px[:, h * H:h * H + H], True, True), "ym%d" % h)
+    wait("y", "qx0")
+    sig(Y.dma_start(T.oc[:, 0:4 * H], u8(qx[:, 0:H])), "st", 16)
+    wait("s", "ym0")
+    sig(S.activation(T.yb[:, 0:H], ps[0][:, 0:H], F.Copy), "yb0")
+    wait("v", "ym1")
+    sig(V.tensor_copy(T.yb[:, H:C], ps[1][:, 0:H]), "yb1")
+    wait("y", "qx1")
+    sig(Y.dma_start(T.oc[:, 4 * H:4 * C], u8(qx[:, H:C])), "st", 16)
+    wait("s", "yb0", "qx1")
+    sig(S.dma_start(T.y[:, 0:H], T.yb[:, 0:H]), "st", 16)
+    for k in range(4):
+        sig((Y if k < 1 else S).dma_start(T.osc[4 * k:4 * k + 4, :], px[32 * k:32 * k + 4, :]), "st", 16)
+    wait("y", "yb1")
+    sig(Y.dma_start(T.y[:, H:C], T.yb[:, H:C]), "st", 16)
+    for name in count:
+        if max([v for (q, m), v in seen.items() if m == name] + [0]) < count[name]:
+            wait("y", name)

@@ -2,9 +2,15 @@ from concourse.mybir import dt, AluOpType as A, ActivationFunctionType as F
 
 C, K, R = 384, 48, 3
 H = C // 2
+HL = 256
 NB = C // 16
-MS = 10
-FW = C + 16
+HB = NB // 2
+TW = 27 * 16
+TB = 3 * 4 * TW
+QT = [0, TW + 128, 2 * TW + 256]
+QZ, QB, QW = 3 * TW + 256, 3 * TW + 256 + H, 3 * TW + 256 + C
+UP = 2.0 ** 15
+U4 = 2.0 ** 13
 MID = (C + K) // 2
 BIG = 2.0 ** 90
 STEP, TINY = 0.6 * 2.0 ** -23, 2.0 ** -125
@@ -17,17 +23,23 @@ SCRATCH = {
     "uq2": ("sbuf", [128, 128], Q4), "up2": ("sbuf", [128, 128], U8),
     "vq": ("sbuf", [128, 128], Q4), "vp": ("sbuf", [128, 128], U8),
     "eq": ("sbuf", [128, 512], Q4), "ep": ("sbuf", [128, 512], U8),
-    "et": ("sbuf", [128, 2048], "bfloat16"), "ones": ("sbuf", [128, 128], "bfloat16"), "ident": ("sbuf", [128, 128], "bfloat16"),
+    "et": ("sbuf", [128, 2048], "bfloat16"), "ones": ("sbuf", [128, 512], "bfloat16"),
+    "b0": ("sbuf", [128, 512], "bfloat16"), "b1": ("sbuf", [128, 512], "bfloat16"), "bq": ("sbuf", [128, 128], Q4), "bp": ("sbuf", [128, 128], U8),
+    "ft": ("sbuf", [128, TB + 4 * H], "bfloat16"), "fq": ("sbuf", [128, QW], Q4), "fp": ("sbuf", [128, QW], U8),
+    "sg": ("sbuf", [128, HB, H + 16], "bfloat16"), "nh": ("sbuf", [128, HB], "float32"), "st16": ("sbuf", [128, H], "bfloat16"),
+    "mk": ("sbuf", [128, C], "bfloat16"), "m16": ("sbuf", [128, 32], "bfloat16"), "m16b": ("sbuf", [128, 16], "bfloat16"),
+    "o16": ("sbuf", [128, NB], "uint16"), "pg": ("sbuf", [128, 8], "float32"),
+    "uu": ("sbuf", [128, NB], "float32"), "ww": ("sbuf", [128, NB], "float32"), "xs": ("sbuf", [128, C], "float32"),
     "pi": ("sbuf", [128, 8], "int32"), "pj": ("sbuf", [128, 8], "int32"), "pf": ("sbuf", [128, 8], "float32"), "pq": ("sbuf", [128, 8], "float32"),
     "ui": ("sbuf", [128, 8], "int32"), "uoff": ("sbuf", [128, 8], "uint16"),
     "n16": ("sbuf", [128, C], "float32"), "tmp": ("sbuf", [128, C], "float32"),
     "cm": ("sbuf", [128, C], "float32"), "cs": ("sbuf", [128, C], "float32"),
     "mask4": ("sbuf", [128, C], "bfloat16"), "keep4": ("sbuf", [128, C], "bfloat16"), "jj": ("sbuf", [128, C], "bfloat16"),
     "xg": ("sbuf", [128, 4 * C], "bfloat16"), "dd": ("sbuf", [128, 4 * C], "bfloat16"),
-    "mm": ("sbuf", [128, C], "float32"), "hh": ("sbuf", [128, C], "float32"), "ee": ("sbuf", [128, C], "float32"), "zz": ("sbuf", [128, 2 * C], "float32"),
-    "ff": ("sbuf", [128, NB, FW], "bfloat16"), "so": ("sbuf", [128, (NB - MS) * FW // 2], "bfloat16"), "cnt": ("sbuf", [128, NB], "float32"),
+    "mm": ("sbuf", [128, C], "float32"), "hh": ("sbuf", [128, C], "float32"), "ee": ("sbuf", [128, H], "float32"), "zz": ("sbuf", [128, C + H], "float32"),
+    "so": ("sbuf", [128, HB, 88], "bfloat16"), "cnt": ("sbuf", [128, HB], "float32"),
     "off": ("sbuf", [128, NB], "uint16"), "oo": ("sbuf", [128, C + K], "bfloat16"),
-    "bm": ("sbuf", [128, K], "bfloat16"), "bs": ("sbuf", [128, K], "bfloat16"),
+    "m4": ("sbuf", [128, K], "bfloat16"), "bs": ("sbuf", [128, K], "float32"), "p4": ("sbuf", [128, 12], "float32"),
     "em": ("sbuf", [128, C], "bfloat16"), "es": ("sbuf", [128, C], "bfloat16"), "xoff": ("sbuf", [128, C // 4], "uint16"),
     "olb": ("sbuf", [128, C], "float32"), "yb": ("sbuf", [128, C], "float32"),
 }
@@ -45,12 +57,13 @@ for _t in range(R):
 for _b in range(8):
     SCRATCH["ps%d" % _b] = ("psum", [128, 512], "float32")
 
-SEMAPHORES = (["lx0", "lx1", "lwc", "lws", "lu", "lv", "st", "snt",
-               "ones", "ident", "etz", "etc", "qe", "gp", "pi", "pf", "pq", "gn16", "gj", "t16", "cm", "vc0", "vc", "mask4",
-               "uoff", "qu", "upk", "qv",
-               "gA", "gB", "qx0", "qx1", "yA", "yB", "qy0", "qy1", "pv0", "pv1", "pz0", "pz1", "m0", "m1", "e0", "e1", "zh", "h1", "eqf",
-               "cA", "cB", "scn", "sA", "sB", "cnt", "offv", "offs", "sct", "bm", "bs", "lst", "em", "es", "xoff", "dM", "dE", "ext", "olb",
-               "ym0", "ym1", "yb0", "yb1"]
+SEMAPHORES = (["lx0", "lx1", "lwc", "lws", "lu", "lv", "st", "snt", "lz",
+               "ones", "fz", "fz0", "qz", "etc", "qe", "gp", "pi", "pf", "pq", "gn16", "gj", "gb0", "gb1", "qb", "t16", "cm", "m16", "m16b", "mk", "pg",
+               "mask4", "uoff", "qu", "upk", "qv",
+               "gA", "gB", "qx0", "qx1", "yA", "yB", "qy0", "qy1", "pv0", "pv1", "pz0", "pz1", "m0", "m1", "e0", "z0", "z1", "zr", "h0", "h1", "nh", "ta", "tb",
+               "st16", "scn", "uu", "cs", "xs", "ww", "off", "sct", "m4", "p4", "bs", "lst", "em", "es", "xoff", "dM", "dE", "ext", "olb",
+               "qfb", "qf0", "qf1", "qf2", "qf3", "ym0", "ym1", "yb0", "yb1"]
+              + ["sg%d" % i for i in range(3)] + ["rl%d" % i for i in range(3)] + ["cb%d" % i for i in range(3)]
               + ["r%d" % i for i in range(8)] + ["aq%d" % i for i in range(R)] + ["al%d" % i for i in range(R)])
 
 
@@ -89,12 +102,13 @@ def rank_program(g, core, T, topo):
     sig(Y.dma_start(T.uin[:], T.u[:]), "lu", 16)
 
     sig(V.memset(T.ones[:], 1.0), "ones")
-    sig(V.memset(T.et[:], 0.0), "etz")
     sig(g.iota(T.pi[:, 0:1], [[1, 1]], 0, 1), "gp")
     sig(g.iota(T.ui[:], [[16, 8]], 0, 0), "gp")
-    wait("g", "ones")
-    sig(g.affine_select(T.ident[:], T.ones[:], [[-1, 128]], A.is_equal, 0.0, 0, 1), "ident")
     sig(g.iota(T.n16[:], [[0, NB], [1, 16]], 0, 0, allow_small_or_imprecise_dtypes=True), "gn16")
+    wait("g", "ones")
+    sig(g.affine_select(T.b0[:], T.ones[:], [[-16, 8], [0, 64]], A.is_ge, 0.0, 0, 1), "gb0")
+    wait("g", "gb0")
+    sig(g.affine_select(T.b1[:], T.b0[:], [[16, 8], [0, 64]], A.is_ge, 0.0, 15, -1), "gb1")
     sig(g.iota(T.jj[:], [[1, C]], -MID, 0, allow_small_or_imprecise_dtypes=True), "gj")
     sig(g.iota(T.oo[:, C:C + K], [[1, K]], C - MID, 0, allow_small_or_imprecise_dtypes=True), "gj")
     wait("v", "gp")
@@ -102,35 +116,53 @@ def rank_program(g, core, T, topo):
     sig(V.tensor_scalar(T.pj[:, 1:2], T.pi[:, 0:1], 12, None, A.bitwise_and), "pi")
     sig(V.tensor_scalar(T.pj[:, 2:3], T.pi[:, 0:1], 3, None, A.bitwise_and), "pi")
     sig(V.tensor_copy(T.uoff[:], T.ui[:]), "uoff")
-    sig(V.memset(T.cs[:], BIG), "vc0")
+    sig(V.memset(T.p4[:, 0:4], 1.0 / U4), "pi")
     wait("v", "pi")
     sig(V.tensor_copy(T.pf[:, 0:1], T.pj[:, 0:1]), "pf")
     sig(V.tensor_scalar(T.pf[:, 1:2], T.pj[:, 1:2], 4.0, None, A.mult), "pf")
-    sig(V.tensor_scalar(T.pf[:, 2:3], T.pj[:, 2:3], float(4 * MID), None, A.add), "pf")
-    sig(V.memset(T.keep4[:], 1.0), "vc0")
+    sig(V.tensor_scalar(T.pf[:, 2:3], T.pj[:, 2:3], 4 * MID + 0.25, None, A.add), "pf")
+    sig(V.tensor_scalar(T.pf[:, 3:4], T.pj[:, 0:1], 15.0, None, A.is_equal), "pf")
+    sig(V.memset(T.ft[:, TB - 192:TB + 4 * H], 0.0), "fz0")
     wait("v", "pf")
     sig(V.tensor_scalar(T.pq[:, 0:4], T.ui[:, 0:4], T.pf[:, 1:2], None, A.is_equal), "pq")
-    wait("v", "vc0")
-    sig(V.memset(T.cs[:, 0:C:16], -BIG), "vc")
-    sig(V.memset(T.keep4[:, 0:C:4], 0.0), "vc")
-    wait("s", "ident", "etz")
-    for b in range(4):
-        sig(S.activation(T.et[:, 512 * b + b:512 * (b + 1):4], T.ident[:], F.Copy), "etc")
-    wait("v", "etc")
-    sig(V.quantize_mx(T.eq[:], T.ep[:], T.et[:]), "qe")
+    sig(V.tensor_scalar(T.p4[:, 4:8], T.ui[:, 0:4], T.pf[:, 1:2], 4.0, A.is_equal, A.mult), "p4")
+    wait("v", "fz0")
+    sig(V.quantize_mx(T.fq[:, QZ:QB], T.fp[:, QZ:QB], T.ft[:, TB:TB + 4 * H]), "qz")
+    wait("v", "gn16")
+    sig(V.tensor_scalar(T.o16[:], T.n16[:, 0:C:16], T.pf[:, 0:1], None, A.add), "m16")
+    wait("s", "ones")
+    for q in (1, 2):
+        sig(S.activation(T.ft[:, 4 * TW * q - 192:4 * TW * q + 192], T.ones[:, 0:C], F.Copy, scale=0.0), "fz")
     wait("s", "pf", "gn16")
     sig(S.activation(T.tmp[:], T.n16[:], F.Abs, bias=T.pf[:, 0:1], scale=-1.0), "t16")
-    wait("s", "pq", "ones")
-    for k in range(4):
-        sig(S.activation(T.mask4[:, k:C:4], T.ones[:, 0:C // 4], F.Copy, scale=T.pq[:, k:k + 1]), "mask4")
+    wait("v", "t16")
+    sig(V.tensor_scalar(T.m16[:, 0:16], T.tmp[:, 0:16], 1.0, UP, A.is_equal, A.mult), "m16")
+    sig(V.tensor_scalar(T.m16[:, 16:32], T.tmp[:, 0:16], 1.0, None, A.min), "m16")
+    sig(V.memset(T.ft[:, 0:192], 0.0), "fz")
+    wait("v", "m16")
+    sig(V.tensor_tensor(T.m16b[:], T.m16[:, 0:16], T.m16[:, 16:32], A.max), "m16b")
+    sig(V.tensor_scalar(T.pg[:, 0:1], T.pf[:, 3:4], 1.0 - UP, UP, A.mult, A.add), "pg")
+    sig(V.tensor_scalar(T.pg[:, 1:2], T.pf[:, 3:4], 1.0 - 1.0 / UP, 1.0 / UP, A.mult, A.add), "pg")
+    sig(V.tensor_scalar(T.pg[:, 2:3], T.pf[:, 0:1], float(H - 16), None, A.add), "pg")
+    sig(V.tensor_scalar(T.pg[:, 3:4], T.pf[:, 0:1], float(H), None, A.add), "pg")
+    wait("v", "p4")
+    sig(V.tensor_tensor_scan(T.p4[:, 8:12], T.p4[:, 0:4], T.p4[:, 4:8], 0.0, A.mult, A.add), "pg")
     wait("s", "t16")
-    sig(S.activation(T.cm[:], T.tmp[:], F.Identity, bias=BIG / 2, scale=-BIG), "cm")
+    sig(S.activation(T.cm[:], T.tmp[:], F.Identity, bias=-BIG / 2, scale=BIG), "cm")
+    wait("s", "m16", "m16b")
+    sig(S.activation(T.mk[:], T.m16b[:].indirect(T.o16[:]), F.Copy), "mk")
+    sig(S.activation(T.cs[:], T.n16[:], F.Identity, bias=BIG, scale=-2 * BIG), "cm")
+    wait("y", "qz", "lwc")
+    for q in (1, 2):
+        sig(Y.dma_start(u8(T.fq[:, QT[q] - 128:QT[q]]), u8(T.fq[:, QZ:QZ + 128])), "lz", 16)
+        sig(Y.dma_start(T.fp[:, QT[q] - 128:QT[q]], T.fp[:, QZ:QZ + 128]), "lz", 16)
     tadd = T.pf[:, 2:3]
 
     def state(t):
         qx, px = T["qx%d" % t], T["px%d" % t]
         src = T.xin if t == 0 else T.xg
-        cuts = [0, 2 * H, 4 * H, 4 * H + 288, 4 * C]
+        h = H if t < R else HL
+        cuts = [0, 2 * h, 4 * h, 4 * h + (288 if t < R else 160), 4 * C]
 
         def pick(i):
             a, b = cuts[i], cuts[i + 1]
@@ -146,11 +178,11 @@ def rank_program(g, core, T, topo):
             pick(1)
             pick(3)
         wait("v", "gA" if t else "lx0")
-        sig(V.quantize_mx(qx[:, 0:H], px[:, 0:H], src[:, 0:4 * H]), "qx0")
+        sig(V.quantize_mx(qx[:, 0:h], px[:, 0:h], src[:, 0:4 * h]), "qx0")
         if t:
             pick(2)
         wait("v", "gB" if t else "lx1")
-        sig(V.quantize_mx(qx[:, H:C], px[:, H:C], src[:, 4 * H:4 * C]), "qx1")
+        sig(V.quantize_mx(qx[:, h:C], px[:, h:C], src[:, 4 * h:4 * C]), "qx1")
 
     for t in range(R):
         qx, px, qy, py, yw = T["qx%d" % t], T["px%d" % t], T["qy%d" % t], T["py%d" % t], T["yw%d" % t]
@@ -200,73 +232,143 @@ def rank_program(g, core, T, topo):
         if t == 0:
             wait("y", "qy1")
             sig(Y.dma_start(T.vin[:], T.v[:]), "lv", 16)
-            wait("v", "cm", "vc", "pf", "mask4", "gj")
-        for h in range(2):
-            a, b = h * H, h * H + H
-            wait("s", "pz%d" % h)
-            sig(S.activation(T.ee[:, a:b], ps[2 * h + 1][:, 0:H], F.Abs, bias=TINY, scale=STEP), "e%d" % h)
-            sig(S.activation(T.zz[:, C + a:C + b], ps[2 * h + 1][:, 0:H], F.Copy), "zh")
+            sig(g.affine_select(T.keep4[:], T.ones[:, 0:C], [[0, C // 4], [1, 4]], A.not_equal, 0.0, 0, 0), "gj")
+            for b in range(4):
+                sig(g.affine_select(T.et[:, 512 * b:512 * (b + 1)], T.ones[:], [[1, 512]], A.is_equal, 0.0, -b, -4), "etc")
+            wait("v", "cm")
+        wait("s", "pz0")
+        sig(S.activation(T.ee[:], ps[1][:, 0:H], F.Abs, bias=TINY, scale=STEP), "e0")
+        sig(S.activation(T.zz[:, 0:H], ps[1][:, 0:H], F.Copy), "z0")
+        wait("s", "pz1")
+        sig(S.activation(T.zz[:, H:C], ps[3][:, 0:H], F.Copy), "z1")
 
         def own(h):
             wait("v", "pv%d" % h)
-            sig(V.tensor_tensor(T.mm[:, h * H:h * H + H], ps[2 * h][:, 0:H], T.cm[:, h * H:h * H + H], A.min), "m%d" % h)
-
-        def lowered(h):
-            wait("v", "pv%d" % h, "e%d" % h)
-            sig(V.tensor_tensor(T.zz[:, h * H:h * H + H], ps[2 * h][:, 0:H], T.ee[:, h * H:h * H + H], A.subtract), "zh")
+            sig(V.tensor_tensor(T.mm[:, h * H:h * H + H], ps[2 * h][:, 0:H], T.cm[:, h * H:h * H + H], A.max), "m%d" % h)
 
         def held(h):
             wait("v", "m%d" % h)
-            sig(V.tensor_tensor_scan(T.hh[:, h * H:h * H + H], T.cs[:, h * H:h * H + H], T.mm[:, h * H:h * H + H], 0.0, A.min, A.max),
-                "h1" if h else "zh")
+            sig(V.tensor_tensor_scan(T.hh[:, h * H:h * H + H], T.cs[:, h * H:h * H + H], T.mm[:, h * H:h * H + H], 0.0, A.max, A.min), "h%d" % h)
+
+        def signs(q):
+            for m in range(4 * q, 4 * q + 4):
+                sig(S.activation(T.sg[:, m, 16:16 + H], T.zz[:, 16 * m + 16:16 * m + 16 + H], F.Sign, bias=T.nh[:, m:m + 1]), "sg%d" % q)
+
+        def relus(q):
+            wait("s", "sg%d" % q, "ta", "fz", "fz0")
+            for k in range(4):
+                a = 4 * TW * q + 65 * k
+                sig(S.activation(T.ft[:, a:a + 4 * (H + 16) - 3:4], T.sg[:, 4 * q + k, :], F.Relu, accum_out=T.cnt[:, 4 * q + k:4 * q + k + 1]), "rl%d" % q)
+
+        def rows(q):
+            for k in range(4):
+                a, m = 4 * TW * q + 65 * k + 64 * 13, HB + 4 * q + k
+                sig(V.tensor_scalar(T.ft[:, a:a + 4 * (H - 16) - 3:4], T.zz[:, 16 * m + 16:16 * m + H], T.hh[:, 16 * m + 15:16 * m + 16], None, A.is_gt),
+                    "cb%d" % q)
+
+        def scans(q):
+            wait("v", "cb%d" % q, "st16")
+            for k in range(4):
+                a, m = 4 * TW * q + 65 * k + 64 * 13, 4 * q + k
+                b = a + 4 * (H - 16) - 3
+                sig(V.tensor_tensor_scan(T.so[:, m, :], T.ft[:, a:b:8], T.ft[:, a + 4:b:8], T.st16[:, 16 * m + 15:16 * m + 16], A.add, A.add), "scn")
+
+        def pack(q, a, b, name):
+            sig(V.quantize_mx(T.fq[:, QT[q] + a:QT[q] + b], T.fp[:, QT[q] + a:QT[q] + b], T.ft[:, 4 * (TW * q + a):4 * (TW * q + b)]), name)
+
+        def colsum(a, w, start=False, stop=False):
+            ins = P.matmul_mx(ps[1][:, 0:w], T.bq[:], T.bp[:], T.fq[:, a:a + w], T.fp[:, a:a + w], start, stop)
+            if stop:
+                sig(ins, "cs")
+
+        def unpack():
+            wait("p", "qe", "aq%d" % t)
+            for b in range(4):
+                sig(P.matmul_mx(ps[4 + b][:, 0:C], T.eq[:, 128 * b:128 * b + 128], T.ep[:, 128 * b:128 * b + 128],
+                                T["lq%d" % t][:], T["lp%d" % t][:], True, True), "dM")
         own(0)
-        lowered(0)
         held(0)
-        lowered(1)
+        wait("v", "e0")
+        sig(V.tensor_tensor(T.zz[:, C:C + H], ps[0][:, 0:H], T.ee[:], A.add), "zr")
+        wait("s", "h0")
+        sig(S.activation(T.nh[:], T.hh[:, 15:H:16], F.Copy, scale=-1.0), "nh")
+        wait("v", "h0")
         own(1)
-        wait("s", "zh")
-        w2 = FW // 2
-        vhalf, shalf = (MS + NB) // 2, MS // 2
-        for m in range(MS):
-            sig(S.activation(T.ff[:, m, 0:C], T.zz[:, 16 * m + 16:16 * m + 16 + C], F.Sign, bias=T.hh[:, 16 * m + 15:16 * m + 16], scale=-1.0),
-                "sA" if m < shalf else "sB")
+        sig(V.tensor_tensor(T.sg[:, :, 0:16], ps[0][:, 0:H], T.hh[:, 0:H], A.is_gt), "ta")
         held(1)
-        wait("v", "zh")
-        for m in range(MS, NB):
-            if m == NB // 2:
-                wait("v", "h1")
-                for h in range(2):
-                    sig(V.tensor_tensor(T.ff[:, h * NB // 2:(h + 1) * NB // 2, C:FW], ps[2 * h][:, 0:H], T.hh[:, h * H:h * H + H], A.is_equal), "eqf")
-            sig(V.tensor_scalar(T.ff[:, m, 0:C], T.zz[:, 16 * m + 16:16 * m + 16 + C], T.hh[:, 16 * m + 15:16 * m + 16], 0.5,
-                                A.is_lt, A.subtract), "cA" if m < vhalf else "cB")
-        for m in range(MS, NB):
-            wait("v", "eqf", "cA" if m < vhalf else "cB")
-            k = m - MS
-            sig(V.tensor_tensor_scan(T.so[:, w2 * k:w2 * k + w2], T.ff[:, m, 0:w2], T.ff[:, m, w2:FW], 0.0, A.add, A.add), "scn")
-        for m in range(MS):
-            wait("s", "eqf", "sA" if m < shalf else "sB")
-            sig(S.activation(T.ff[:, m, :], T.ff[:, m, :], F.Relu, accum_out=T.cnt[:, m:m + 1]), "cnt")
-        wait("p", "qe", "aq%d" % t)
-        for b in range(4):
-            sig(P.matmul_mx(ps[4 + b][:, 0:C], T.eq[:, 128 * b:128 * b + 128], T.ep[:, 128 * b:128 * b + 128],
-                            T["lq%d" % t][:], T["lp%d" % t][:], True, True), "dM")
+        wait("s", "nh", "z0", "z1")
+        signs(0)
+        signs(1)
+        relus(0)
+        signs(2)
+        relus(1)
+        relus(2)
+        if t == 0:
+            wait("v", "gb1")
+            sig(V.quantize_mx(T.bq[:], T.bp[:], T.b1[:]), "qb")
+            wait("v", "qz", "mk", "fz")
+        wait("v", "h1", "z1", "zr")
+        sig(V.tensor_tensor(T.ft[:, TB:TB + 4 * H:4], ps[2][:, 0:H], T.hh[:, H:C], A.is_gt), "tb")
+        rows(0)
+        wait("v", "tb")
+        sig(V.tensor_tensor_scan(T.st16[:], T.mk[:, 0:H], T.ft[:, TB:TB + 4 * H:4], 0.0, A.mult, A.add), "st16")
+        sig(V.quantize_mx(T.fq[:, QB:QW], T.fp[:, QB:QW], T.ft[:, TB:TB + 4 * H]), "qfb")
+        rows(1)
+        scans(0)
+        rows(2)
+        scans(1)
+        wait("v", "rl0")
+        pack(0, 0, TW, "qf0")
+        wait("v", "cb2")
+        pack(2, 256, TW, "qf2")
+        scans(2)
+        wait("v", "rl1")
+        pack(1, 0, TW, "qf1")
+        wait("v", "rl2")
+        pack(2, 0, 256, "qf3")
+        wait("v", "pg", "scn")
+        sig(V.tensor_scalar(T.uu[:, 0:HB], T.cnt[:], T.pg[:, 2:3], T.pg[:, 0:1], A.add, A.mult), "uu")
+        sig(V.tensor_scalar(T.uu[:, HB:NB], T.so[:, :, 87], T.pg[:, 3:4], T.pg[:, 0:1], A.add, A.mult), "uu")
+        wait("p", "qb", "lz", "e0", "z0", "qfb")
+        colsum(QZ, C, start=True)
+        if t:
+            unpack()
+        wait("p", "qf0")
+        colsum(0, C)
+        colsum(C, 128)
+        wait("p", "qf2")
+        colsum(QT[2] + 256, TW - 256)
+        wait("p", "qf1")
+        colsum(QT[1] - 64, C)
+        colsum(QT[1] - 64 + C, 128)
+        wait("p", "qf3")
+        colsum(QT[2] - 128, C, stop=True)
+        if t == 0:
+            wait("v", "etc")
+            sig(V.quantize_mx(T.eq[:], T.ep[:], T.et[:]), "qe")
+            unpack()
+            wait("s", "pq")
+            for k in range(4):
+                sig(S.activation(T.mask4[:, k:C:4], T.ones[:, 0:C // 4], F.Copy, scale=T.pq[:, k:k + 1]), "mask4")
+            wait("s", "mask4")
+            sig(S.activation(T.m4[:], T.mask4[:, 0:K], F.Identity, bias=U4, scale=-U4), "m4")
         wait("s", "dM")
         for b in range(4):
             sig(S.activation(T.dd[:, b:4 * C:4], ps[4 + b][:, 0:C], F.Copy), "dE")
-        wait("v", "scn")
-        sig(V.tensor_scalar(T.off[:, MS:NB], T.so[:, w2 - 1:w2 * (NB - MS):w2], -1.0, float(C // 2), A.mult, A.add), "offv")
-        wait("v", "offv")
-        sig(V.tensor_copy(T.oo[:, 0:C].indirect(T.off[:, MS:NB]), T.jj[:, 16 * MS:C]), "sct")
-        wait("v", "cnt")
-        sig(V.tensor_scalar(T.off[:, 0:MS], T.cnt[:, 0:MS], -1.0, float(C), A.mult, A.add), "offs")
-        wait("v", "offs", "sct")
-        sig(V.tensor_copy(T.oo[:, 0:C].indirect(T.off[:, 0:MS]), T.jj[:, 0:16 * MS]), "sct")
+        wait("v", "cs")
+        sig(V.tensor_tensor_scan(T.xs[:], T.mk[:], ps[1][:, 0:C], 0.0, A.mult, A.add), "xs")
+        wait("v", "xs", "uu")
+        sig(V.tensor_tensor(T.ww[:], T.uu[:], T.xs[:, 15:C:16], A.subtract), "ww")
+        wait("v", "ww")
+        sig(V.tensor_scalar(T.off[:], T.ww[:], T.pg[:, 1:2], 0.25, A.mult, A.add), "off")
+        wait("v", "off", "gj")
+        sig(V.tensor_copy(T.oo[:, 0:C].indirect(T.off[:]), T.jj[:]), "sct")
+        if t == 0:
+            wait("v", "mask4", "m4")
         wait("v", "sct")
-        sig(V.tensor_tensor(T.bm[:], T.oo[:, 0:K], T.mask4[:, 0:K], A.mult), "bm")
-        wait("v", "bm")
-        sig(V.tensor_tensor_scan(T.bs[:], T.keep4[:, 0:K], T.bm[:], 0.0, A.mult, A.add), "bs")
+        sig(V.tensor_tensor_scan(T.bs[:], T.m4[:], T.oo[:, 0:K], 0.0, A.mult, A.add), "bs")
         wait("v", "bs")
-        sig(V.tensor_scalar(T["lst%d" % t][:], T.bs[:, 3:K:4], 4.0, tadd, A.mult, A.add), "lst")
+        sig(V.tensor_scalar(T["lst%d" % t][:], T.bs[:, 3:K:4], T.p4[:, 11:12], tadd, A.mult, A.add), "lst")
         wait("g", "lst")
         g.remote_dma(T["ll%d" % t][:], T["lst%d" % t][:], T.sem["al%d" % t], T.sem.snt, pid, rid, mask)
         count["snt"] += ne
@@ -293,23 +395,23 @@ def rank_program(g, core, T, topo):
     state(R)
     qx, px = T["qx%d" % R], T["px%d" % R]
     wait("p", "qv")
-    for h in range(2):
+    for h, (a, b) in enumerate(((0, HL), (HL, C))):
         wait("p", "qx%d" % h)
-        sig(P.matmul_mx(ps[h][:, 0:H], T.vq[:], T.vp[:], qx[:, h * H:h * H + H], px[:, h * H:h * H + H], True, True), "ym%d" % h)
+        sig(P.matmul_mx(ps[h][:, 0:b - a], T.vq[:], T.vp[:], qx[:, a:b], px[:, a:b], True, True), "ym%d" % h)
     wait("y", "qx0")
-    sig(Y.dma_start(T.oc[:, 0:4 * H], u8(qx[:, 0:H])), "st", 16)
+    sig(Y.dma_start(T.oc[:, 0:4 * HL], u8(qx[:, 0:HL])), "st", 16)
     wait("s", "ym0")
-    sig(S.activation(T.yb[:, 0:H], ps[0][:, 0:H], F.Copy), "yb0")
+    sig(S.activation(T.yb[:, 0:HL], ps[0][:, 0:HL], F.Copy), "yb0")
     wait("v", "ym1")
-    sig(V.tensor_copy(T.yb[:, H:C], ps[1][:, 0:H]), "yb1")
+    sig(V.tensor_copy(T.yb[:, HL:C], ps[1][:, 0:C - HL]), "yb1")
     wait("y", "qx1")
-    sig(Y.dma_start(T.oc[:, 4 * H:4 * C], u8(qx[:, H:C])), "st", 16)
+    sig(Y.dma_start(T.oc[:, 4 * HL:4 * C], u8(qx[:, HL:C])), "st", 16)
     wait("s", "yb0", "qx1")
-    sig(S.dma_start(T.y[:, 0:H], T.yb[:, 0:H]), "st", 16)
+    sig(S.dma_start(T.y[:, 0:HL], T.yb[:, 0:HL]), "st", 16)
     for k in range(4):
         sig((Y if k < 1 else S).dma_start(T.osc[4 * k:4 * k + 4, :], px[32 * k:32 * k + 4, :]), "st", 16)
     wait("y", "yb1")
-    sig(Y.dma_start(T.y[:, H:C], T.yb[:, H:C]), "st", 16)
+    sig(Y.dma_start(T.y[:, HL:C], T.yb[:, HL:C]), "st", 16)
     for name in count:
         if max([v for (q, m), v in seen.items() if m == name] + [0]) < count[name]:
             wait("y", name)

@@ -2,18 +2,19 @@ from concourse.mybir import dt, AluOpType as A, ActivationFunctionType as F
 
 C, K, R = 384, 48, 3
 H = C // 2
-HL = 256
 NB = C // 16
 HB = NB // 2
-TW = 27 * 16
-TB = 3 * 4 * TW
-QT = [0, TW + 128, 2 * TW + 256]
-QZ, QB, QW = 3 * TW + 256, 3 * TW + 256 + H, 3 * TW + 256 + C
+CB = 11
+NT = 5
+LO = [0, 2, 4, 6, 8]
+TWD = [16 * (NB - 2 * a) for a in LO]
+FT = [4 * sum(TWD[:q]) for q in range(NT + 1)]
+QT = [0, 416, 800, 1152, 1472]
+QW = QT[4] + 128
 UP = 2.0 ** 15
 U4 = 2.0 ** 13
 MID = (C + K) // 2
 BIG = 2.0 ** 90
-STEP, TINY = 0.6 * 2.0 ** -23, 2.0 ** -125
 Q4, U8 = "float8_e4m3fn_x4", "uint8"
 
 SCRATCH = {
@@ -25,19 +26,19 @@ SCRATCH = {
     "eq": ("sbuf", [128, 512], Q4), "ep": ("sbuf", [128, 512], U8),
     "et": ("sbuf", [128, 2048], "bfloat16"), "ones": ("sbuf", [128, 512], "bfloat16"),
     "b0": ("sbuf", [128, 512], "bfloat16"), "b1": ("sbuf", [128, 512], "bfloat16"), "bq": ("sbuf", [128, 128], Q4), "bp": ("sbuf", [128, 128], U8),
-    "ft": ("sbuf", [128, TB + 4 * H], "bfloat16"), "fq": ("sbuf", [128, QW], Q4), "fp": ("sbuf", [128, QW], U8),
-    "sg": ("sbuf", [128, HB, H + 16], "bfloat16"), "nh": ("sbuf", [128, HB], "float32"), "st16": ("sbuf", [128, H], "bfloat16"),
+    "ft": ("sbuf", [128, FT[NT]], "bfloat16"), "fq": ("sbuf", [128, QW], Q4), "fp": ("sbuf", [128, QW], U8),
+    "sg": ("sbuf", [128, HB, C], "bfloat16"), "st16": ("sbuf", [128, C], "bfloat16"), "vb": ("sbuf", [128, 64], "bfloat16"),
     "mk": ("sbuf", [128, C], "bfloat16"), "m16": ("sbuf", [128, 32], "bfloat16"), "m16b": ("sbuf", [128, 16], "bfloat16"),
-    "o16": ("sbuf", [128, NB], "uint16"), "pg": ("sbuf", [128, 8], "float32"),
-    "uu": ("sbuf", [128, NB], "float32"), "ww": ("sbuf", [128, NB], "float32"), "xs": ("sbuf", [128, C], "float32"),
-    "pi": ("sbuf", [128, 8], "int32"), "pj": ("sbuf", [128, 8], "int32"), "pf": ("sbuf", [128, 8], "float32"), "pq": ("sbuf", [128, 8], "float32"),
-    "ui": ("sbuf", [128, 8], "int32"), "uoff": ("sbuf", [128, 8], "uint16"),
-    "n16": ("sbuf", [128, C], "float32"), "tmp": ("sbuf", [128, C], "float32"),
-    "cm": ("sbuf", [128, C], "float32"), "cs": ("sbuf", [128, C], "float32"),
+    "o16": ("sbuf", [128, NB], "uint16"), "pg": ("sbuf", [128, 8], "float32"), "ni": ("sbuf", [128, NB], "float32"), "nv": ("sbuf", [128, NB], "float32"),
+    "u1": ("sbuf", [128, NB], "float32"), "uv": ("sbuf", [128, NB], "float32"), "ww": ("sbuf", [128, NB], "float32"), "xs": ("sbuf", [128, C], "float32"),
+    "pi": ("sbuf", [128, 8], "int32"), "pj": ("sbuf", [128, 8], "int32"), "pf": ("sbuf", [128, 8], "float32"),
+    "uoff": ("sbuf", [128, 8], "uint16"),
+    "n16": ("sbuf", [128, H], "float32"), "tmp": ("sbuf", [128, H], "float32"),
+    "cm": ("sbuf", [128, H], "float32"), "cs": ("sbuf", [128, H], "float32"),
     "mask4": ("sbuf", [128, C], "bfloat16"), "keep4": ("sbuf", [128, C], "bfloat16"), "jj": ("sbuf", [128, C], "bfloat16"),
     "xg": ("sbuf", [128, 4 * C], "bfloat16"), "dd": ("sbuf", [128, 4 * C], "bfloat16"),
-    "mm": ("sbuf", [128, C], "float32"), "hh": ("sbuf", [128, C], "float32"), "ee": ("sbuf", [128, H], "float32"), "zz": ("sbuf", [128, C + H], "float32"),
-    "so": ("sbuf", [128, HB, 88], "bfloat16"), "cnt": ("sbuf", [128, HB], "float32"),
+    "mm": ("sbuf", [128, C], "float32"), "hh": ("sbuf", [128, C], "float32"), "zz": ("sbuf", [128, C], "float32"),
+    "so": ("sbuf", [128, NB, 176], "float16"), "cnt": ("sbuf", [128, HB], "float32"), "cn2": ("sbuf", [128, 15 - CB], "float32"),
     "off": ("sbuf", [128, NB], "uint16"), "oo": ("sbuf", [128, C + K], "bfloat16"),
     "m4": ("sbuf", [128, K], "bfloat16"), "bs": ("sbuf", [128, K], "float32"), "p4": ("sbuf", [128, 12], "float32"),
     "em": ("sbuf", [128, C], "bfloat16"), "es": ("sbuf", [128, C], "bfloat16"), "xoff": ("sbuf", [128, C // 4], "uint16"),
@@ -57,13 +58,13 @@ for _t in range(R):
 for _b in range(8):
     SCRATCH["ps%d" % _b] = ("psum", [128, 512], "float32")
 
-SEMAPHORES = (["lx0", "lx1", "lwc", "lws", "lu", "lv", "st", "snt", "lz",
-               "ones", "fz", "fz0", "qz", "etc", "qe", "gp", "pi", "pf", "pq", "gn16", "gj", "gb0", "gb1", "qb", "t16", "cm", "m16", "m16b", "mk", "pg",
-               "mask4", "uoff", "qu", "upk", "qv",
-               "gA", "gB", "qx0", "qx1", "yA", "yB", "qy0", "qy1", "pv0", "pv1", "pz0", "pz1", "m0", "m1", "e0", "z0", "z1", "zr", "h0", "h1", "nh", "ta", "tb",
-               "st16", "scn", "uu", "cs", "xs", "ww", "off", "sct", "m4", "p4", "bs", "lst", "em", "es", "xoff", "dM", "dE", "ext", "olb",
-               "qfb", "qf0", "qf1", "qf2", "qf3", "ym0", "ym1", "yb0", "yb1"]
-              + ["sg%d" % i for i in range(3)] + ["rl%d" % i for i in range(3)] + ["cb%d" % i for i in range(3)]
+SEMAPHORES = (["lx0", "lx1", "lwc", "lz", "lws", "lu", "lv", "st", "snt",
+               "ones", "etz", "fz", "fz0", "qz", "etc", "qe", "gp", "gu", "pi0", "pf0", "pi", "pq", "gn16", "gj", "gb0", "gb1", "qb", "t16",
+               "cm", "m16", "mk", "pg", "mask4", "qu", "upk", "qv",
+               "gA", "gB", "qx0", "qx1", "yA", "yB", "qy0", "qy1", "pv0", "pv1", "pz0", "pz1", "m0", "m1", "z", "h0", "h1", "u2",
+               "st16", "scn", "u1", "uu", "csm", "xs", "ww", "off", "sct", "m4", "p4", "bs", "lst", "em", "es", "dE", "ext", "olb",
+               "ym0", "ym1", "yb0", "yb1", "m16b"]
+              + ["sg%d" % i for i in range(6)] + ["f%d" % i for i in range(NT)] + ["qf%d" % i for i in range(NT)]
               + ["r%d" % i for i in range(8)] + ["aq%d" % i for i in range(R)] + ["al%d" % i for i in range(R)])
 
 
@@ -95,276 +96,297 @@ def rank_program(g, core, T, topo):
 
     ps = [T["ps%d" % b] for b in range(8)]
 
-    sig(Y.dma_start(T.xin[:, 0:4 * H], T.x[:, 0:4 * H]), "lx0", 16)
+    sig(Y.dma_start(T.xin[:, 4 * H:4 * C], T.x[:, 4 * H:4 * C]), "lx1", 16)
     sig(S.dma_start(T.wp[:], T.ws[:]), "lws", 16)
     sig(Y.dma_start(u8(T.wq[:]), T.wc[:]), "lwc", 16)
-    sig(S.dma_start(T.xin[:, 4 * H:4 * C], T.x[:, 4 * H:4 * C]), "lx1", 16)
+    sig(S.dma_start(T.xin[:, 0:4 * H], T.x[:, 0:4 * H]), "lx0", 16)
     sig(Y.dma_start(T.uin[:], T.u[:]), "lu", 16)
 
     sig(V.memset(T.ones[:], 1.0), "ones")
-    sig(g.iota(T.pi[:, 0:1], [[1, 1]], 0, 1), "gp")
-    sig(g.iota(T.ui[:], [[16, 8]], 0, 0), "gp")
-    sig(g.iota(T.n16[:], [[0, NB], [1, 16]], 0, 0, allow_small_or_imprecise_dtypes=True), "gn16")
+    sig(g.iota(T.pi[:, 0:5], [[-4, 5]], 16, 1), "gp")
+    sig(g.iota(T.n16[:], [[0, HB], [1, 16]], 0, 0, allow_small_or_imprecise_dtypes=True), "gn16")
     wait("g", "ones")
     sig(g.affine_select(T.b0[:], T.ones[:], [[-16, 8], [0, 64]], A.is_ge, 0.0, 0, 1), "gb0")
     wait("g", "gb0")
     sig(g.affine_select(T.b1[:], T.b0[:], [[16, 8], [0, 64]], A.is_ge, 0.0, 15, -1), "gb1")
     sig(g.iota(T.jj[:], [[1, C]], -MID, 0, allow_small_or_imprecise_dtypes=True), "gj")
-    sig(g.iota(T.oo[:, C:C + K], [[1, K]], C - MID, 0, allow_small_or_imprecise_dtypes=True), "gj")
+    sig(V.memset(T.ft[:, FT[4] - 128:FT[5]], 0.0), "fz0")
     wait("v", "gp")
-    sig(V.tensor_scalar(T.pj[:, 0:1], T.pi[:, 0:1], 15, None, A.bitwise_and), "pi")
-    sig(V.tensor_scalar(T.pj[:, 1:2], T.pi[:, 0:1], 12, None, A.bitwise_and), "pi")
-    sig(V.tensor_scalar(T.pj[:, 2:3], T.pi[:, 0:1], 3, None, A.bitwise_and), "pi")
-    sig(V.tensor_copy(T.uoff[:], T.ui[:]), "uoff")
-    sig(V.memset(T.p4[:, 0:4], 1.0 / U4), "pi")
-    wait("v", "pi")
-    sig(V.tensor_copy(T.pf[:, 0:1], T.pj[:, 0:1]), "pf")
-    sig(V.tensor_scalar(T.pf[:, 1:2], T.pj[:, 1:2], 4.0, None, A.mult), "pf")
-    sig(V.tensor_scalar(T.pf[:, 2:3], T.pj[:, 2:3], 4 * MID + 0.25, None, A.add), "pf")
-    sig(V.tensor_scalar(T.pf[:, 3:4], T.pj[:, 0:1], 15.0, None, A.is_equal), "pf")
-    sig(V.memset(T.ft[:, TB - 192:TB + 4 * H], 0.0), "fz0")
-    wait("v", "pf")
-    sig(V.tensor_scalar(T.pq[:, 0:4], T.ui[:, 0:4], T.pf[:, 1:2], None, A.is_equal), "pq")
-    sig(V.tensor_scalar(T.p4[:, 4:8], T.ui[:, 0:4], T.pf[:, 1:2], 4.0, A.is_equal, A.mult), "p4")
+    sig(V.tensor_scalar(T.pj[:, 4:5], T.pi[:, 4:5], 15, None, A.bitwise_and), "pi0")
+    sig(V.memset(T.ft[:, 0:64], 0.0), "fz")
+    wait("v", "pi0")
+    sig(V.tensor_copy(T.pf[:, 0:1], T.pj[:, 4:5]), "pf0")
+    sig(V.tensor_scalar(T.pf[:, 3:4], T.pj[:, 4:5], 15.0, None, A.is_equal), "pq")
     wait("v", "fz0")
-    sig(V.quantize_mx(T.fq[:, QZ:QB], T.fp[:, QZ:QB], T.ft[:, TB:TB + 4 * H]), "qz")
-    wait("v", "gn16")
-    sig(V.tensor_scalar(T.o16[:], T.n16[:, 0:C:16], T.pf[:, 0:1], None, A.add), "m16")
+    sig(V.quantize_mx(T.fq[:, QT[4] - 128:QT[4]], T.fp[:, QT[4] - 128:QT[4]], T.ft[:, FT[4]:FT[5]]), "qz")
     wait("s", "ones")
-    for q in (1, 2):
-        sig(S.activation(T.ft[:, 4 * TW * q - 192:4 * TW * q + 192], T.ones[:, 0:C], F.Copy, scale=0.0), "fz")
-    wait("s", "pf", "gn16")
+    for q in range(1, 4):
+        sig(S.activation(T.ft[:, FT[q] - 128:FT[q] + 64], T.ones[:, 0:192], F.Copy, scale=0.0), "fz")
+    wait("s", "gn16")
+    sig(S.activation(T.cs[:], T.n16[:], F.Identity, bias=BIG, scale=-2 * BIG), "cm")
+    wait("s", "pf0")
     sig(S.activation(T.tmp[:], T.n16[:], F.Abs, bias=T.pf[:, 0:1], scale=-1.0), "t16")
-    wait("v", "t16")
-    sig(V.tensor_scalar(T.m16[:, 0:16], T.tmp[:, 0:16], 1.0, UP, A.is_equal, A.mult), "m16")
-    sig(V.tensor_scalar(T.m16[:, 16:32], T.tmp[:, 0:16], 1.0, None, A.min), "m16")
-    sig(V.memset(T.ft[:, 0:192], 0.0), "fz")
-    wait("v", "m16")
-    sig(V.tensor_tensor(T.m16b[:], T.m16[:, 0:16], T.m16[:, 16:32], A.max), "m16b")
-    sig(V.tensor_scalar(T.pg[:, 0:1], T.pf[:, 3:4], 1.0 - UP, UP, A.mult, A.add), "pg")
-    sig(V.tensor_scalar(T.pg[:, 1:2], T.pf[:, 3:4], 1.0 - 1.0 / UP, 1.0 / UP, A.mult, A.add), "pg")
-    sig(V.tensor_scalar(T.pg[:, 2:3], T.pf[:, 0:1], float(H - 16), None, A.add), "pg")
-    sig(V.tensor_scalar(T.pg[:, 3:4], T.pf[:, 0:1], float(H), None, A.add), "pg")
-    wait("v", "p4")
-    sig(V.tensor_tensor_scan(T.p4[:, 8:12], T.p4[:, 0:4], T.p4[:, 4:8], 0.0, A.mult, A.add), "pg")
     wait("s", "t16")
     sig(S.activation(T.cm[:], T.tmp[:], F.Identity, bias=-BIG / 2, scale=BIG), "cm")
-    wait("s", "m16", "m16b")
-    sig(S.activation(T.mk[:], T.m16b[:].indirect(T.o16[:]), F.Copy), "mk")
-    sig(S.activation(T.cs[:], T.n16[:], F.Identity, bias=BIG, scale=-2 * BIG), "cm")
-    wait("y", "qz", "lwc")
-    for q in (1, 2):
-        sig(Y.dma_start(u8(T.fq[:, QT[q] - 128:QT[q]]), u8(T.fq[:, QZ:QZ + 128])), "lz", 16)
-        sig(Y.dma_start(T.fp[:, QT[q] - 128:QT[q]], T.fp[:, QZ:QZ + 128]), "lz", 16)
+    wait("y", "qz", "lu")
+    for b in range(4):
+        sig(Y.dma_start(T.et[:, 512 * b:512 * b + 512], T.ft[:, FT[4]:FT[5]]), "etz", 16)
+    for q in range(1, 4):
+        w = 32 * q
+        sig(Y.dma_start(u8(T.fq[:, QT[q] - w:QT[q]]), u8(T.fq[:, QT[4] - w:QT[4]])), "lz", 16)
+        sig(Y.dma_start(T.fp[:, QT[q] - w:QT[q]], T.fp[:, QT[4] - w:QT[4]]), "lz", 16)
+    wait("v", "pq", "pf0")
+    sig(V.tensor_scalar(T.pg[:, 1:2], T.pf[:, 3:4], 1.0 - 1.0 / UP, 1.0 / UP, A.mult, A.add), "scn")
+    sig(V.tensor_scalar(T.pg[:, 2:3], T.pf[:, 0:1], 0.25, None, A.add), "scn")
+    sig(V.memset(T.so[:, CB:NB, 175], 0.0), "scn")
     tadd = T.pf[:, 2:3]
+
+    def pick(t, q, a, b, name):
+        w = T["yw%d" % (t - 1)][:].indirect(T.xoff[:, a // 16:b // 16])
+        sig(V.tensor_copy(T.xg[:, a:b], w) if q == "v" else S.activation(T.xg[:, a:b], w, F.Copy), name)
 
     def state(t):
         qx, px = T["qx%d" % t], T["px%d" % t]
-        src = T.xin if t == 0 else T.xg
-        h = H if t < R else HL
-        cuts = [0, 2 * h, 4 * h, 4 * h + (288 if t < R else 160), 4 * C]
-
-        def pick(i):
-            a, b = cuts[i], cuts[i + 1]
-            w = T["yw%d" % (t - 1)][:].indirect(T.xoff[:, a // 16:b // 16])
-            if i % 2 == 0:
-                sig(V.tensor_copy(T.xg[:, a:b], w), "gA" if i < 2 else "gB")
-            else:
-                sig(S.activation(T.xg[:, a:b], w, F.Copy), "gA" if i < 2 else "gB")
-        if t:
-            wait("v", "xoff", "ext")
-            wait("s", "xoff", "ext")
-            pick(0)
-            pick(1)
-            pick(3)
-        wait("v", "gA" if t else "lx0")
-        sig(V.quantize_mx(qx[:, 0:h], px[:, 0:h], src[:, 0:4 * h]), "qx0")
-        if t:
-            pick(2)
-        wait("v", "gB" if t else "lx1")
-        sig(V.quantize_mx(qx[:, h:C], px[:, h:C], src[:, 4 * h:4 * C]), "qx1")
+        wait("v", "ext")
+        wait("s", "ext")
+        pick(t, "v", 4 * H, 6 * H, "gA")
+        pick(t, "s", 6 * H, 8 * H, "gA")
+        pick(t, "s", 288, 4 * H, "gB")
+        wait("v", "gA")
+        sig(V.quantize_mx(qx[:, H:C], px[:, H:C], T.xg[:, 4 * H:4 * C]), "qx1")
+        pick(t, "v", 0, 288, "gB")
+        wait("v", "gB")
+        sig(V.quantize_mx(qx[:, 0:H], px[:, 0:H], T.xg[:, 0:4 * H]), "qx0")
 
     for t in range(R):
         qx, px, qy, py, yw = T["qx%d" % t], T["px%d" % t], T["qy%d" % t], T["py%d" % t], T["yw%d" % t]
-        state(t)
-        wait("p", "lwc", "lws")
-        for h in range(2):
-            wait("p", "qx%d" % h)
-            for b in ((2, 0, 3, 1) if h == 0 else (0, 1, 3, 2)):
+
+        def layer(h, order):
+            wait("p", "qx%d" % h, "lws", "lwc")
+            for b in order:
                 sig(P.matmul_mx(ps[4 * h + b][:, 0:H], T.wq[:, 128 * b:128 * b + 128], T.wp[:, 128 * b:128 * b + 128],
                                 qx[:, h * H:h * H + H], px[:, h * H:h * H + H], True, True), "r%d" % (4 * h + b))
-        if t == 0:
-            wait("v", "lu", "uoff")
-            sig(V.quantize_mx(T.uq[:], T.up[:], T.uin[:]), "qu")
 
         def evac(q, h, b):
             wait(q, "r%d" % (4 * h + b))
             o, i = yw[:, 4 * H * h + b:4 * H * (h + 1):4], ps[4 * h + b][:, 0:H]
             ins = V.tensor_scalar(o, i, 0.03125, None, A.mult) if q == "v" else S.activation(o, i, F.Copy, scale=0.03125)
             sig(ins, "yB" if h else "yA")
-        evac("v", 0, 0)
-        evac("s", 0, 2)
-        evac("v", 0, 1)
-        evac("s", 0, 3)
+
+        def qx_half(h):
+            wait("v", "lx%d" % h)
+            sig(V.quantize_mx(qx[:, h * H:h * H + H], px[:, h * H:h * H + H], T.xin[:, 4 * h * H:4 * (h * H + H)]), "qx%d" % h)
+
+        def qy_half(h):
+            wait("v", "yB" if h else "yA")
+            sig(V.quantize_mx(qy[:, h * H:h * H + H], py[:, h * H:h * H + H], yw[:, 4 * h * H:4 * (h * H + H)]), "qy%d" % h)
+
+        def scores(h):
+            wait("p", "upk", "qy%d" % h)
+            for k in ((0, 1) if h == 1 else (1, 0)):
+                sig(P.matmul_mx(ps[4 * h + k][:, 0:H], T.uq2[:], T.up2[:], qy[:, h * H:h * H + H], py[:, h * H:h * H + H], True, True),
+                    ("pv%d" if k == 0 else "pz%d") % h)
+        if t == 0:
+            qx_half(1)
+            sig(V.tensor_scalar(T.pj[:, 0:4], T.pi[:, 0:4], 12, None, A.bitwise_and), "pi")
+            sig(V.tensor_scalar(T.pj[:, 5:6], T.pi[:, 4:5], 3, None, A.bitwise_and), "pi")
+            sig(V.memset(T.p4[:, 0:4], 1.0 / U4), "pi")
+            qx_half(0)
+        else:
+            state(t)
+        layer(1, (2, 0, 3, 1))
+        layer(0, (0, 1, 3, 2))
+        if t == 0:
+            wait("v", "t16")
+            sig(V.tensor_scalar(T.uoff[:], T.n16[:, 0:8], 16.0, None, A.mult), "qu")
+            sig(V.tensor_scalar(T.m16[:, 0:16], T.tmp[:, 0:16], 1.0, UP, A.is_equal, A.mult), "m16")
+            sig(V.tensor_scalar(T.m16[:, 16:32], T.tmp[:, 0:16], 1.0, None, A.min), "m16")
+            sig(V.tensor_scalar(T.o16[:], T.n16[:, 0:NB], 0.0, T.pf[:, 0:1], A.mult, A.add), "m16b")
+            wait("v", "pi")
+            sig(V.tensor_scalar(T.p4[:, 4:8], T.pj[:, 0:4], 0.0, 4.0, A.is_equal, A.mult), "p4")
+            sig(V.tensor_scalar(T.pf[:, 2:3], T.pj[:, 5:6], 4 * MID + 0.25, None, A.add), "pg")
+            wait("v", "lu")
+            sig(V.quantize_mx(T.uq[:], T.up[:], T.uin[:]), "qu")
+            wait("v", "m16")
+            sig(V.tensor_tensor(T.m16b[:], T.m16[:, 0:16], T.m16[:, 16:32], A.max), "m16b")
+        evac("v", 1, 0)
+        evac("s", 1, 2)
+        if t == 0:
+            wait("v", "p4")
+            sig(V.tensor_tensor_scan(T.p4[:, 8:12], T.p4[:, 0:4], T.p4[:, 4:8], 0.0, A.mult, A.add), "pg")
+        evac("v", 1, 1)
+        evac("s", 1, 3)
         if t == 0:
             wait("v", "qu")
             sig(V.tensor_copy(T.uq2[:].bitcast(dt.uint32), T.uq[:].bitcast(dt.uint32).indirect(T.uoff[:])), "upk")
-            sig(V.tensor_copy(T.up2[:], T.up[:].indirect(T.uoff[:])), "upk")
-        wait("v", "yA")
-        sig(V.quantize_mx(qy[:, 0:H], py[:, 0:H], yw[:, 0:4 * H]), "qy0")
-        evac("s", 1, 0)
-        evac("v", 1, 3)
-        evac("s", 1, 1)
-        evac("s", 1, 2)
-        wait("v", "yB")
-        sig(V.quantize_mx(qy[:, H:C], py[:, H:C], yw[:, 4 * H:4 * C]), "qy1")
-        wait("p", "upk")
-        for h in range(2):
-            wait("p", "qy%d" % h)
-            for k in (1, 0):
-                sig(P.matmul_mx(ps[2 * h + k][:, 0:H], T.uq2[:], T.up2[:], qy[:, h * H:h * H + H], py[:, h * H:h * H + H], True, True),
-                    ("pv%d" if k == 0 else "pz%d") % h)
+            wait("s", "qu")
+            sig(S.activation(T.up2[:], T.up[:].indirect(T.uoff[:]), F.Copy), "upk")
+        qy_half(1)
+        evac("s", 0, 0)
+        evac("s", 0, 1)
+        evac("s", 0, 3)
+        evac("v", 0, 2)
+        if t == 0:
+            wait("s", "m16b")
+            sig(S.activation(T.mk[:], T.m16b[:].indirect(T.o16[:]), F.Copy), "mk")
+        qy_half(0)
+        scores(1)
+        scores(0)
         wait("g", "qy0", "qy1")
         g.remote_dma(u8(T["lq%d" % t][:]), u8(qy[:]), T.sem["aq%d" % t], T.sem.snt, pid, rid, mask)
         g.remote_dma(T["lp%d" % t][:], py[:], T.sem["aq%d" % t], T.sem.snt, pid, rid, mask)
         count["snt"] = count.get("snt", 0) + 2 * ne
         count["aq%d" % t] = 2 * ne
         if t == 0:
-            wait("y", "qy1")
+            wait("y", "qy0")
             sig(Y.dma_start(T.vin[:], T.v[:]), "lv", 16)
-            sig(g.affine_select(T.keep4[:], T.ones[:, 0:C], [[0, C // 4], [1, 4]], A.not_equal, 0.0, 0, 0), "gj")
+            wait("g", "etz")
             for b in range(4):
-                sig(g.affine_select(T.et[:, 512 * b:512 * (b + 1)], T.ones[:], [[1, 512]], A.is_equal, 0.0, -b, -4), "etc")
+                sig(g.affine_select(T.et[:, 512 * b + b:512 * (b + 1):4], T.ones[:, 0:128], [[-1, 128]], A.is_equal, 0.0, 0, 1), "etc")
+            sig(g.affine_select(T.keep4[:], T.ones[:, 0:C], [[0, C // 4], [1, 4]], A.not_equal, 0.0, 0, 0), "gu")
             wait("v", "cm")
-        wait("s", "pz0")
-        sig(S.activation(T.ee[:], ps[1][:, 0:H], F.Abs, bias=TINY, scale=STEP), "e0")
-        sig(S.activation(T.zz[:, 0:H], ps[1][:, 0:H], F.Copy), "z0")
-        wait("s", "pz1")
-        sig(S.activation(T.zz[:, H:C], ps[3][:, 0:H], F.Copy), "z1")
+        for h in (1, 0):
+            wait("s", "pz%d" % h)
+            sig(S.activation(T.zz[:, h * H:h * H + H], ps[4 * h + 1][:, 0:H], F.Copy), "z")
 
         def own(h):
             wait("v", "pv%d" % h)
-            sig(V.tensor_tensor(T.mm[:, h * H:h * H + H], ps[2 * h][:, 0:H], T.cm[:, h * H:h * H + H], A.max), "m%d" % h)
+            sig(V.tensor_tensor(T.mm[:, h * H:h * H + H], ps[4 * h][:, 0:H], T.cm[:], A.max), "m%d" % h)
 
         def held(h):
             wait("v", "m%d" % h)
-            sig(V.tensor_tensor_scan(T.hh[:, h * H:h * H + H], T.cs[:, h * H:h * H + H], T.mm[:, h * H:h * H + H], 0.0, A.max, A.min), "h%d" % h)
+            sig(V.tensor_tensor_scan(T.hh[:, h * H:h * H + H], T.cs[:], T.mm[:, h * H:h * H + H], 0.0, A.max, A.min), "h%d" % h)
+
+        def inrun(h):
+            wait("v", "h%d" % h)
+            sig(V.tensor_tensor(T.ft[:, 4 * H * h + 3:4 * H * (h + 1):4], ps[4 * h][:, 0:H], T.hh[:, h * H:h * H + H], A.is_gt), "f0")
 
         def signs(q):
-            for m in range(4 * q, 4 * q + 4):
-                sig(S.activation(T.sg[:, m, 16:16 + H], T.zz[:, 16 * m + 16:16 * m + 16 + H], F.Sign, bias=T.nh[:, m:m + 1]), "sg%d" % q)
+            for m in (NB - 1 - 2 * q, NB - 2 - 2 * q):
+                lo, hi = (NB - 1 - m, m) if q < 4 else (CB, m if m == 15 else 16)
+                sig(S.activation(T.sg[:, m - HB, 16 * lo:16 * hi], T.zz[:, 16 * lo:16 * hi], F.Sign, bias=T.hh[:, 16 * m + 15:16 * m + 16], scale=-1.0),
+                    "sg%d" % q)
 
-        def relus(q):
-            wait("s", "sg%d" % q, "ta", "fz", "fz0")
-            for k in range(4):
-                a = 4 * TW * q + 65 * k
-                sig(S.activation(T.ft[:, a:a + 4 * (H + 16) - 3:4], T.sg[:, 4 * q + k, :], F.Relu, accum_out=T.cnt[:, 4 * q + k:4 * q + k + 1]), "rl%d" % q)
+        def flags(q):
+            wait("s", "sg%d" % q, "fz", "fz0")
+            for k in range(2):
+                m = NB - 1 - 2 * q - k
+                lo = NB - 1 - m if q < 4 else CB
+                i, a = T.sg[:, m - HB, 16 * lo:16 * m], FT[min(q, 3)] + 65 * k
+                o = T.ft[:, a:a + 64 * (m - lo) - 3:4] if q < 4 else i
+                sig(S.activation(o, i, F.Sign, bias=1.0, scale=-1.0, accum_out=T.cnt[:, m - HB:m - HB + 1]), "f%d" % q if q < 4 else "u1")
+                if q > 3 and m < 15:
+                    i = T.sg[:, m - HB, 16 * m + 16:256]
+                    sig(S.activation(i, i, F.Relu, scale=-1.0, accum_out=T.cn2[:, m - CB:m - CB + 1]), "u1")
+
+        def first(q):
+            if q == 4:
+                return [(m, FT[4] + 65 * (m - 7), 16 * (15 - m)) for m in range(7, CB)]
+            return [(lo - 1, FT[q] + 64 * (lo - LO[q]) + 2 + (lo % 2 if q else 0), C - 32 * lo) for lo in (2 * q, 2 * q + 1) if lo]
 
         def rows(q):
-            for k in range(4):
-                a, m = 4 * TW * q + 65 * k + 64 * 13, HB + 4 * q + k
-                sig(V.tensor_scalar(T.ft[:, a:a + 4 * (H - 16) - 3:4], T.zz[:, 16 * m + 16:16 * m + H], T.hh[:, 16 * m + 15:16 * m + 16], None, A.is_gt),
-                    "cb%d" % q)
+            for m, a, w in first(q):
+                sig(V.tensor_scalar(T.ft[:, a:a + 4 * w - 3:4], T.zz[:, 16 * m + 16:16 * m + 16 + w], T.hh[:, 16 * m + 15:16 * m + 16], None, A.is_gt),
+                    "f%d" % q)
 
         def scans(q):
-            wait("v", "cb%d" % q, "st16")
-            for k in range(4):
-                a, m = 4 * TW * q + 65 * k + 64 * 13, 4 * q + k
-                b = a + 4 * (H - 16) - 3
-                sig(V.tensor_tensor_scan(T.so[:, m, :], T.ft[:, a:b:8], T.ft[:, a + 4:b:8], T.st16[:, 16 * m + 15:16 * m + 16], A.add, A.add), "scn")
+            for m, a, w in first(q):
+                b = a + 4 * w - 3
+                sig(V.tensor_tensor_scan(T.so[:, m, 176 - w // 2:176], T.ft[:, a:b:8], T.ft[:, a + 4:b:8], 0.0, A.add, A.add), "scn")
 
-        def pack(q, a, b, name):
-            sig(V.quantize_mx(T.fq[:, QT[q] + a:QT[q] + b], T.fp[:, QT[q] + a:QT[q] + b], T.ft[:, 4 * (TW * q + a):4 * (TW * q + b)]), name)
+        def pack(q):
+            wait("v", "f%d" % q)
+            sig(V.quantize_mx(T.fq[:, QT[q]:QT[q] + TWD[q]], T.fp[:, QT[q]:QT[q] + TWD[q]], T.ft[:, FT[q]:FT[q + 1]]), "qf%d" % q)
+            wait("p", "qf%d" % q)
+            a, e = QT[q] - 16 * LO[q], QT[q] + TWD[q]
+            ins = P.matmul_mx(ps[2][:, 0:e - a], T.bq[:], T.bp[:], T.fq[:, a:e], T.fp[:, a:e], q == 0, q == 3)
+            if q == 3:
+                sig(ins, "csm")
 
-        def colsum(a, w, start=False, stop=False):
-            ins = P.matmul_mx(ps[1][:, 0:w], T.bq[:], T.bp[:], T.fq[:, a:a + w], T.fp[:, a:a + w], start, stop)
-            if stop:
-                sig(ins, "cs")
-
-        def unpack():
-            wait("p", "qe", "aq%d" % t)
-            for b in range(4):
-                sig(P.matmul_mx(ps[4 + b][:, 0:C], T.eq[:, 128 * b:128 * b + 128], T.ep[:, 128 * b:128 * b + 128],
-                                T["lq%d" % t][:], T["lp%d" % t][:], True, True), "dM")
+        own(1)
+        held(1)
+        if t == 0:
+            wait("v", "fz")
+        inrun(1)
         own(0)
         held(0)
-        wait("v", "e0")
-        sig(V.tensor_tensor(T.zz[:, C:C + H], ps[0][:, 0:H], T.ee[:], A.add), "zr")
-        wait("s", "h0")
-        sig(S.activation(T.nh[:], T.hh[:, 15:H:16], F.Copy, scale=-1.0), "nh")
-        wait("v", "h0")
-        own(1)
-        sig(V.tensor_tensor(T.sg[:, :, 0:16], ps[0][:, 0:H], T.hh[:, 0:H], A.is_gt), "ta")
-        held(1)
-        wait("s", "nh", "z0", "z1")
+        wait("s", "h1", "z")
         signs(0)
-        signs(1)
-        relus(0)
-        signs(2)
-        relus(1)
-        relus(2)
+        for q in range(3):
+            signs(q + 1)
+            flags(q)
+        flags(3)
+        signs(4)
+        wait("s", "h0")
+        sig(S.activation(T.vb[:], T.zz[:, H:256], F.Sign, bias=T.hh[:, H - 1:H], scale=-1.0), "sg5")
+        signs(5)
+        flags(4)
+        flags(5)
+        sig(S.activation(T.vb[:], T.vb[:], F.Relu, scale=-1.0, accum_out=T.cn2[:, 0:1]), "u1")
         if t == 0:
             wait("v", "gb1")
             sig(V.quantize_mx(T.bq[:], T.bp[:], T.b1[:]), "qb")
-            wait("v", "qz", "mk", "fz")
-        wait("v", "h1", "z1", "zr")
-        sig(V.tensor_tensor(T.ft[:, TB:TB + 4 * H:4], ps[2][:, 0:H], T.hh[:, H:C], A.is_gt), "tb")
-        rows(0)
-        wait("v", "tb")
-        sig(V.tensor_tensor_scan(T.st16[:], T.mk[:, 0:H], T.ft[:, TB:TB + 4 * H:4], 0.0, A.mult, A.add), "st16")
-        sig(V.quantize_mx(T.fq[:, QB:QW], T.fp[:, QB:QW], T.ft[:, TB:TB + 4 * H]), "qfb")
-        rows(1)
-        scans(0)
-        rows(2)
+        inrun(0)
+        wait("v", "z")
+        for q in range(4):
+            rows(q)
+        wait("p", "qb", "qz")
+        pack(0)
+        wait("v", "etz")
+        rows(4)
+        wait("p", "lz")
+        pack(1)
+        pack(4)
         scans(1)
-        wait("v", "rl0")
-        pack(0, 0, TW, "qf0")
-        wait("v", "cb2")
-        pack(2, 256, TW, "qf2")
-        scans(2)
-        wait("v", "rl1")
-        pack(1, 0, TW, "qf1")
-        wait("v", "rl2")
-        pack(2, 0, 256, "qf3")
-        wait("v", "pg", "scn")
-        sig(V.tensor_scalar(T.uu[:, 0:HB], T.cnt[:], T.pg[:, 2:3], T.pg[:, 0:1], A.add, A.mult), "uu")
-        sig(V.tensor_scalar(T.uu[:, HB:NB], T.so[:, :, 87], T.pg[:, 3:4], T.pg[:, 0:1], A.add, A.mult), "uu")
-        wait("p", "qb", "lz", "e0", "z0", "qfb")
-        colsum(QZ, C, start=True)
-        if t:
-            unpack()
-        wait("p", "qf0")
-        colsum(0, C)
-        colsum(C, 128)
-        wait("p", "qf2")
-        colsum(QT[2] + 256, TW - 256)
-        wait("p", "qf1")
-        colsum(QT[1] - 64, C)
-        colsum(QT[1] - 64 + C, 128)
-        wait("p", "qf3")
-        colsum(QT[2] - 128, C, stop=True)
+        wait("v", "mk")
+        sig(V.tensor_tensor_scan(T.st16[:], T.mk[:], T.ft[:, 3:4 * C:4], 0.0, A.mult, A.add), "st16")
+        if t == 0:
+            wait("v", "gj")
+            sig(V.tensor_scalar(T.ni[:, 0:8], T.jj[:, 0:128:16], 2.0, 2.0 * MID + 16, A.mult, A.add), "st16")
+            sig(V.tensor_scalar(T.ni[:, 8:CB], T.jj[:, 128:16 * CB:16], MID + 128.0, None, A.add), "st16")
+            sig(V.memset(T.ni[:, CB:16], 16.0 * (8 + CB)), "st16")
+            sig(V.tensor_scalar(T.ni[:, 16:NB], T.jj[:, 256:C:16], -2.0, 736.0 - 2 * MID, A.mult, A.add), "st16")
+        pack(2)
+        wait("v", "st16")
+        sig(V.tensor_tensor(T.nv[:], T.st16[:, 15:C:16], T.ni[:], A.add), "scn")
+        pack(3)
+        for q in (2, 4, 3, 0):
+            scans(q)
         if t == 0:
             wait("v", "etc")
             sig(V.quantize_mx(T.eq[:], T.ep[:], T.et[:]), "qe")
-            unpack()
-            wait("s", "pq")
-            for k in range(4):
-                sig(S.activation(T.mask4[:, k:C:4], T.ones[:, 0:C // 4], F.Copy, scale=T.pq[:, k:k + 1]), "mask4")
-            wait("s", "mask4")
-            sig(S.activation(T.m4[:], T.mask4[:, 0:K], F.Identity, bias=U4, scale=-U4), "m4")
-        wait("s", "dM")
+        wait("v", "scn")
+        sig(V.tensor_tensor(T.uv[:], T.so[:, :, 175], T.nv[:], A.add), "u1")
+        wait("v", "csm")
+        sig(V.tensor_tensor_scan(T.xs[:], T.mk[:], ps[2][:, 0:C], 0.0, A.mult, A.add), "xs")
+        wait("v", "u1")
+        sig(V.tensor_tensor(T.uv[:, HB:NB], T.uv[:, HB:NB], T.cnt[:], A.add), "u2")
+        wait("v", "xs")
+        sig(V.tensor_scalar(T.u1[:], T.xs[:, 15:C:16], T.pg[:, 1:2], T.pg[:, 2:3], A.mult, A.subtract), "uu")
+        wait("v", "u2")
+        sig(V.tensor_tensor(T.uv[:, CB:15], T.uv[:, CB:15], T.cn2[:], A.add), "uu")
+        wait("p", "qe", "aq%d" % t)
         for b in range(4):
+            sig(P.matmul_mx(ps[4 + b][:, 0:C], T.eq[:, 128 * b:128 * b + 128], T.ep[:, 128 * b:128 * b + 128],
+                            T["lq%d" % t][:], T["lp%d" % t][:], True, True), "r%d" % (4 + b))
+        if t == 0:
+            wait("s", "p4", "gj")
+            for k in range(4):
+                sig(S.activation(T.mask4[:, k:C:4], T.ones[:, 0:C // 4], F.Copy, scale=T.p4[:, 4 + k:5 + k]), "mask4")
+            sig(S.activation(T.oo[:, C:C + K], T.jj[:, 0:K], F.Identity, bias=float(C)), "m4")
+            wait("s", "mask4")
+            sig(S.activation(T.m4[:], T.mask4[:, 0:K], F.Identity, bias=U4, scale=-U4 / 4), "m4")
+        for b in range(4):
+            wait("s", "r%d" % (4 + b))
             sig(S.activation(T.dd[:, b:4 * C:4], ps[4 + b][:, 0:C], F.Copy), "dE")
-        wait("v", "cs")
-        sig(V.tensor_tensor_scan(T.xs[:], T.mk[:], ps[1][:, 0:C], 0.0, A.mult, A.add), "xs")
-        wait("v", "xs", "uu")
-        sig(V.tensor_tensor(T.ww[:], T.uu[:], T.xs[:, 15:C:16], A.subtract), "ww")
+        wait("v", "uu")
+        sig(V.tensor_tensor(T.ww[:], T.uv[:], T.u1[:], A.subtract), "ww")
         wait("v", "ww")
-        sig(V.tensor_scalar(T.off[:], T.ww[:], T.pg[:, 1:2], 0.25, A.mult, A.add), "off")
-        wait("v", "off", "gj")
+        sig(V.tensor_copy(T.off[:], T.ww[:]), "off")
+        wait("v", "off")
         sig(V.tensor_copy(T.oo[:, 0:C].indirect(T.off[:]), T.jj[:]), "sct")
         if t == 0:
-            wait("v", "mask4", "m4")
+            wait("v", "m4", "pg", "gu")
         wait("v", "sct")
         sig(V.tensor_tensor_scan(T.bs[:], T.m4[:], T.oo[:, 0:K], 0.0, A.mult, A.add), "bs")
         wait("v", "bs")
@@ -377,7 +399,7 @@ def rank_program(g, core, T, topo):
         wait("v", "em")
         sig(V.tensor_tensor_scan(T.es[:], T.keep4[:], T.em[:], 0.0, A.mult, A.add), "es")
         wait("v", "es")
-        sig(V.tensor_scalar(T.xoff[:], T.es[:, 3:C:4], 4.0, tadd, A.mult, A.add), "xoff")
+        sig(V.tensor_scalar(T.xoff[:], T.es[:, 3:C:4], tadd, None, A.add), "ext")
         if t == 0:
             wait("v", "lv")
             sig(V.quantize_mx(T.vq[:], T.vp[:], T.vin[:]), "qv")
@@ -395,23 +417,24 @@ def rank_program(g, core, T, topo):
     state(R)
     qx, px = T["qx%d" % R], T["px%d" % R]
     wait("p", "qv")
-    for h, (a, b) in enumerate(((0, HL), (HL, C))):
+    for h in (1, 0):
         wait("p", "qx%d" % h)
-        sig(P.matmul_mx(ps[h][:, 0:b - a], T.vq[:], T.vp[:], qx[:, a:b], px[:, a:b], True, True), "ym%d" % h)
-    wait("y", "qx0")
-    sig(Y.dma_start(T.oc[:, 0:4 * HL], u8(qx[:, 0:HL])), "st", 16)
-    wait("s", "ym0")
-    sig(S.activation(T.yb[:, 0:HL], ps[0][:, 0:HL], F.Copy), "yb0")
-    wait("v", "ym1")
-    sig(V.tensor_copy(T.yb[:, HL:C], ps[1][:, 0:C - HL]), "yb1")
+        sig(P.matmul_mx(ps[h][:, 0:H], T.vq[:], T.vp[:], qx[:, h * H:h * H + H], px[:, h * H:h * H + H], True, True), "ym%d" % h)
     wait("y", "qx1")
-    sig(Y.dma_start(T.oc[:, 4 * HL:4 * C], u8(qx[:, HL:C])), "st", 16)
-    wait("s", "yb0", "qx1")
-    sig(S.dma_start(T.y[:, 0:HL], T.yb[:, 0:HL]), "st", 16)
-    for k in range(4):
-        sig((Y if k < 1 else S).dma_start(T.osc[4 * k:4 * k + 4, :], px[32 * k:32 * k + 4, :]), "st", 16)
+    sig(Y.dma_start(T.oc[:, 4 * H:4 * C], u8(qx[:, H:C])), "st", 16)
+    wait("s", "ym1")
+    sig(S.activation(T.yb[:, H:C], ps[1][:, 0:H], F.Copy), "yb1")
+    wait("v", "ym0")
+    sig(V.tensor_copy(T.yb[:, 0:H], ps[0][:, 0:H]), "yb0")
     wait("y", "yb1")
-    sig(Y.dma_start(T.y[:, HL:C], T.yb[:, HL:C]), "st", 16)
+    sig(Y.dma_start(T.y[:, H:C], T.yb[:, H:C]), "st", 16)
+    wait("y", "qx0")
+    sig(Y.dma_start(T.oc[:, 0:4 * H], u8(qx[:, 0:H])), "st", 16)
+    wait("s", "qx0", "qx1")
+    for k in range(4):
+        sig(S.dma_start(T.osc[4 * k:4 * k + 4, :], px[32 * k:32 * k + 4, :]), "st", 16)
+    wait("y", "yb0")
+    sig(Y.dma_start(T.y[:, 0:H], T.yb[:, 0:H]), "st", 16)
     for name in count:
         if max([v for (q, m), v in seen.items() if m == name] + [0]) < count[name]:
             wait("y", name)

from concourse.mybir import dt, AluOpType as A, ActivationFunctionType as F

C, K, R = 384, 48, 3
H = C // 2
NB = C // 16
HB = NB // 2
CB = 11
NT = 5
LO = [0, 2, 4, 6, 8]
TWD = [16 * (NB - 2 * a) for a in LO]
FT = [4 * sum(TWD[:q]) for q in range(NT + 1)]
QT = [0, 416, 800, 1152, 1472]
QW = QT[4] + 128
UP = 2.0 ** 15
U4 = 2.0 ** 13
MID = (C + K) // 2
BIG = 2.0 ** 90
Q4, U8 = "float8_e4m3fn_x4", "uint8"

SCRATCH = {
    "xin": ("sbuf", [128, 4 * C], "bfloat16"), "uin": ("sbuf", [128, 512], "bfloat16"), "vin": ("sbuf", [128, 512], "bfloat16"),
    "wq": ("sbuf", [128, 512], Q4), "wp": ("sbuf", [128, 512], U8),
    "uq": ("sbuf", [128, 128], Q4), "up": ("sbuf", [128, 128], U8),
    "uq2": ("sbuf", [128, 128], Q4), "up2": ("sbuf", [128, 128], U8),
    "vq": ("sbuf", [128, 128], Q4), "vp": ("sbuf", [128, 128], U8),
    "eq": ("sbuf", [128, 512], Q4), "ep": ("sbuf", [128, 512], U8),
    "et": ("sbuf", [128, 2048], "bfloat16"), "ones": ("sbuf", [128, 512], "bfloat16"),
    "b0": ("sbuf", [128, 512], "bfloat16"), "b1": ("sbuf", [128, 512], "bfloat16"), "bq": ("sbuf", [128, 128], Q4), "bp": ("sbuf", [128, 128], U8),
    "ft": ("sbuf", [128, FT[NT]], "bfloat16"), "fq": ("sbuf", [128, QW], Q4), "fp": ("sbuf", [128, QW], U8),
    "sg": ("sbuf", [128, HB, C], "bfloat16"), "st16": ("sbuf", [128, C], "bfloat16"), "vb": ("sbuf", [128, 64], "bfloat16"),
    "mk": ("sbuf", [128, C], "bfloat16"), "m16": ("sbuf", [128, 32], "bfloat16"), "m16b": ("sbuf", [128, 16], "bfloat16"),
    "o16": ("sbuf", [128, NB], "uint16"), "pg": ("sbuf", [128, 8], "float32"), "ni": ("sbuf", [128, NB], "float32"), "nv": ("sbuf", [128, NB], "float32"),
    "u1": ("sbuf", [128, NB], "float32"), "uv": ("sbuf", [128, NB], "float32"), "ww": ("sbuf", [128, NB], "float32"), "xs": ("sbuf", [128, C], "float32"),
    "pi": ("sbuf", [128, 8], "int32"), "pj": ("sbuf", [128, 8], "int32"), "pf": ("sbuf", [128, 8], "float32"),
    "uoff": ("sbuf", [128, 8], "uint16"),
    "n16": ("sbuf", [128, H], "float32"), "tmp": ("sbuf", [128, H], "float32"),
    "cm": ("sbuf", [128, H], "float32"), "cs": ("sbuf", [128, H], "float32"),
    "mask4": ("sbuf", [128, C], "bfloat16"), "keep4": ("sbuf", [128, C], "bfloat16"), "jj": ("sbuf", [128, C], "bfloat16"),
    "xg": ("sbuf", [128, 4 * C], "bfloat16"), "dd": ("sbuf", [128, 4 * C], "bfloat16"),
    "mm": ("sbuf", [128, C], "float32"), "hh": ("sbuf", [128, C], "float32"), "zz": ("sbuf", [128, C], "float32"),
    "so": ("sbuf", [128, NB, 176], "float16"), "cnt": ("sbuf", [128, HB], "float32"), "cn2": ("sbuf", [128, 15 - CB], "float32"),
    "off": ("sbuf", [128, NB], "uint16"), "oo": ("sbuf", [128, C + K], "bfloat16"),
    "m4": ("sbuf", [128, K], "bfloat16"), "bs": ("sbuf", [128, K], "float32"), "p4": ("sbuf", [128, 12], "float32"),
    "em": ("sbuf", [128, C], "bfloat16"), "es": ("sbuf", [128, C], "bfloat16"), "xoff": ("sbuf", [128, C // 4], "uint16"),
    "olb": ("sbuf", [128, C], "float32"), "yb": ("sbuf", [128, C], "float32"),
}
for _t in range(R + 1):
    SCRATCH["qx%d" % _t] = ("sbuf", [128, C], Q4)
    SCRATCH["px%d" % _t] = ("sbuf", [128, C], U8)
for _t in range(R):
    SCRATCH["yw%d" % _t] = ("sbuf", [128, 4 * (C + K)], "bfloat16")
    SCRATCH["qy%d" % _t] = ("sbuf", [128, C], Q4)
    SCRATCH["py%d" % _t] = ("sbuf", [128, C], U8)
    SCRATCH["lq%d" % _t] = ("sbuf", [128, C], Q4)
    SCRATCH["lp%d" % _t] = ("sbuf", [128, C], U8)
    SCRATCH["lst%d" % _t] = ("sbuf", [128, K // 4], "uint16")
    SCRATCH["ll%d" % _t] = ("sbuf", [128, K // 4], "uint16")
for _b in range(8):
    SCRATCH["ps%d" % _b] = ("psum", [128, 512], "float32")

SEMAPHORES = (["lx0", "lx1", "lwc", "lz", "lws", "lu", "lv", "st", "snt",
               "ones", "etz", "fz", "fz0", "qz", "etc", "qe", "gp", "gu", "pi0", "pf0", "pi", "pq", "gn16", "gj", "gb0", "gb1", "qb", "t16",
               "cm", "m16", "mk", "pg", "mask4", "qu", "upk", "qv",
               "gA", "gB", "qx0", "qx1", "yA", "yB", "qy0", "qy1", "pv0", "pv1", "pz0", "pz1", "m0", "m1", "z", "h0", "h1", "u2",
               "st16", "scn", "u1", "uu", "csm", "xs", "ww", "off", "sct", "m4", "p4", "bs", "lst", "em", "es", "dE", "ext", "olb",
               "ym0", "ym1", "yb0", "yb1", "m16b"]
              + ["sg%d" % i for i in range(6)] + ["f%d" % i for i in range(NT)] + ["qf%d" % i for i in range(NT)]
              + ["r%d" % i for i in range(8)] + ["aq%d" % i for i in range(R)] + ["al%d" % i for i in range(R)])


def rank_program(g, core, T, topo):
    rank = T.rank_of(core)
    if rank is None:
        return
    n = len(T.cores)
    dst = T.cores[(rank - 1) % n]
    rid, pid = topo.addr(dst)[0], topo.addr(dst)[1]
    mask = topo.mask(core, dst)
    ne = len(topo.engines(core, dst))
    V, S, P, Y = g.vector, g.scalar, g.tensor, g.sync
    qn = {"g": g, "v": V, "s": S, "p": P, "y": Y}
    count, seen = {}, {}

    def sig(ins, name, k=1):
        ins.then_inc(T.sem[name], k)
        count[name] = count.get(name, 0) + k

    def wait(q, *names):
        for name in names:
            if seen.get((q, name), 0) < count[name]:
                qn[q].wait_ge(T.sem[name], count[name])
                seen[(q, name)] = count[name]

    def u8(v):
        return v.bitcast(dt.uint8)

    ps = [T["ps%d" % b] for b in range(8)]

    sig(Y.dma_start(T.xin[:, 4 * H:4 * C], T.x[:, 4 * H:4 * C]), "lx1", 16)
    sig(S.dma_start(T.wp[:], T.ws[:]), "lws", 16)
    sig(Y.dma_start(u8(T.wq[:]), T.wc[:]), "lwc", 16)
    sig(S.dma_start(T.xin[:, 0:4 * H], T.x[:, 0:4 * H]), "lx0", 16)
    sig(Y.dma_start(T.uin[:], T.u[:]), "lu", 16)

    sig(V.memset(T.ones[:], 1.0), "ones")
    sig(g.iota(T.pi[:, 0:5], [[-4, 5]], 16, 1), "gp")
    sig(g.iota(T.n16[:], [[0, HB], [1, 16]], 0, 0, allow_small_or_imprecise_dtypes=True), "gn16")
    wait("g", "ones")
    sig(g.affine_select(T.b0[:], T.ones[:], [[-16, 8], [0, 64]], A.is_ge, 0.0, 0, 1), "gb0")
    wait("g", "gb0")
    sig(g.affine_select(T.b1[:], T.b0[:], [[16, 8], [0, 64]], A.is_ge, 0.0, 15, -1), "gb1")
    sig(g.iota(T.jj[:], [[1, C]], -MID, 0, allow_small_or_imprecise_dtypes=True), "gj")
    sig(V.memset(T.ft[:, FT[4] - 128:FT[5]], 0.0), "fz0")
    wait("v", "gp")
    sig(V.tensor_scalar(T.pj[:, 4:5], T.pi[:, 4:5], 15, None, A.bitwise_and), "pi0")
    sig(V.memset(T.ft[:, 0:64], 0.0), "fz")
    wait("v", "pi0")
    sig(V.tensor_copy(T.pf[:, 0:1], T.pj[:, 4:5]), "pf0")
    sig(V.tensor_scalar(T.pf[:, 3:4], T.pj[:, 4:5], 15.0, None, A.is_equal), "pq")
    wait("v", "fz0")
    sig(V.quantize_mx(T.fq[:, QT[4] - 128:QT[4]], T.fp[:, QT[4] - 128:QT[4]], T.ft[:, FT[4]:FT[5]]), "qz")
    wait("s", "ones")
    for q in range(1, 4):
        sig(S.activation(T.ft[:, FT[q] - 128:FT[q] + 64], T.ones[:, 0:192], F.Copy, scale=0.0), "fz")
    wait("s", "gn16")
    sig(S.activation(T.cs[:], T.n16[:], F.Identity, bias=BIG, scale=-2 * BIG), "cm")
    wait("s", "pf0")
    sig(S.activation(T.tmp[:], T.n16[:], F.Abs, bias=T.pf[:, 0:1], scale=-1.0), "t16")
    wait("s", "t16")
    sig(S.activation(T.cm[:], T.tmp[:], F.Identity, bias=-BIG / 2, scale=BIG), "cm")
    wait("y", "qz", "lu")
    for b in range(4):
        sig(Y.dma_start(T.et[:, 512 * b:512 * b + 512], T.ft[:, FT[4]:FT[5]]), "etz", 16)
    for q in range(1, 4):
        w = 32 * q
        sig(Y.dma_start(u8(T.fq[:, QT[q] - w:QT[q]]), u8(T.fq[:, QT[4] - w:QT[4]])), "lz", 16)
        sig(Y.dma_start(T.fp[:, QT[q] - w:QT[q]], T.fp[:, QT[4] - w:QT[4]]), "lz", 16)
    wait("v", "pq", "pf0")
    sig(V.tensor_scalar(T.pg[:, 1:2], T.pf[:, 3:4], 1.0 - 1.0 / UP, 1.0 / UP, A.mult, A.add), "scn")
    sig(V.tensor_scalar(T.pg[:, 2:3], T.pf[:, 0:1], 0.25, None, A.add), "scn")
    sig(V.memset(T.so[:, CB:NB, 175], 0.0), "scn")
    tadd = T.pf[:, 2:3]

    def pick(t, q, a, b, name):
        w = T["yw%d" % (t - 1)][:].indirect(T.xoff[:, a // 16:b // 16])
        sig(V.tensor_copy(T.xg[:, a:b], w) if q == "v" else S.activation(T.xg[:, a:b], w, F.Copy), name)

    def state(t):
        qx, px = T["qx%d" % t], T["px%d" % t]
        wait("v", "ext")
        wait("s", "ext")
        pick(t, "v", 4 * H, 6 * H, "gA")
        pick(t, "s", 6 * H, 8 * H, "gA")
        pick(t, "s", 288, 4 * H, "gB")
        wait("v", "gA")
        sig(V.quantize_mx(qx[:, H:C], px[:, H:C], T.xg[:, 4 * H:4 * C]), "qx1")
        pick(t, "v", 0, 288, "gB")
        wait("v", "gB")
        sig(V.quantize_mx(qx[:, 0:H], px[:, 0:H], T.xg[:, 0:4 * H]), "qx0")

    for t in range(R):
        qx, px, qy, py, yw = T["qx%d" % t], T["px%d" % t], T["qy%d" % t], T["py%d" % t], T["yw%d" % t]

        def layer(h, order):
            wait("p", "qx%d" % h, "lws", "lwc")
            for b in order:
                sig(P.matmul_mx(ps[4 * h + b][:, 0:H], T.wq[:, 128 * b:128 * b + 128], T.wp[:, 128 * b:128 * b + 128],
                                qx[:, h * H:h * H + H], px[:, h * H:h * H + H], True, True), "r%d" % (4 * h + b))

        def evac(q, h, b):
            wait(q, "r%d" % (4 * h + b))
            o, i = yw[:, 4 * H * h + b:4 * H * (h + 1):4], ps[4 * h + b][:, 0:H]
            ins = V.tensor_scalar(o, i, 0.03125, None, A.mult) if q == "v" else S.activation(o, i, F.Copy, scale=0.03125)
            sig(ins, "yB" if h else "yA")

        def qx_half(h):
            wait("v", "lx%d" % h)
            sig(V.quantize_mx(qx[:, h * H:h * H + H], px[:, h * H:h * H + H], T.xin[:, 4 * h * H:4 * (h * H + H)]), "qx%d" % h)

        def qy_half(h):
            wait("v", "yB" if h else "yA")
            sig(V.quantize_mx(qy[:, h * H:h * H + H], py[:, h * H:h * H + H], yw[:, 4 * h * H:4 * (h * H + H)]), "qy%d" % h)

        def scores(h):
            wait("p", "upk", "qy%d" % h)
            for k in ((0, 1) if h == 1 else (1, 0)):
                sig(P.matmul_mx(ps[4 * h + k][:, 0:H], T.uq2[:], T.up2[:], qy[:, h * H:h * H + H], py[:, h * H:h * H + H], True, True),
                    ("pv%d" if k == 0 else "pz%d") % h)
        if t == 0:
            qx_half(1)
            sig(V.tensor_scalar(T.pj[:, 0:4], T.pi[:, 0:4], 12, None, A.bitwise_and), "pi")
            sig(V.tensor_scalar(T.pj[:, 5:6], T.pi[:, 4:5], 3, None, A.bitwise_and), "pi")
            sig(V.memset(T.p4[:, 0:4], 1.0 / U4), "pi")
            qx_half(0)
        else:
            state(t)
        layer(1, (2, 0, 3, 1))
        layer(0, (0, 1, 3, 2))
        if t == 0:
            wait("v", "t16")
            sig(V.tensor_scalar(T.uoff[:], T.n16[:, 0:8], 16.0, None, A.mult), "qu")
            sig(V.tensor_scalar(T.m16[:, 0:16], T.tmp[:, 0:16], 1.0, UP, A.is_equal, A.mult), "m16")
            sig(V.tensor_scalar(T.m16[:, 16:32], T.tmp[:, 0:16], 1.0, None, A.min), "m16")
            sig(V.tensor_scalar(T.o16[:], T.n16[:, 0:NB], 0.0, T.pf[:, 0:1], A.mult, A.add), "m16b")
            wait("v", "pi")
            sig(V.tensor_scalar(T.p4[:, 4:8], T.pj[:, 0:4], 0.0, 4.0, A.is_equal, A.mult), "p4")
            sig(V.tensor_scalar(T.pf[:, 2:3], T.pj[:, 5:6], 4 * MID + 0.25, None, A.add), "pg")
            wait("v", "lu")
            sig(V.quantize_mx(T.uq[:], T.up[:], T.uin[:]), "qu")
            wait("v", "m16")
            sig(V.tensor_tensor(T.m16b[:], T.m16[:, 0:16], T.m16[:, 16:32], A.max), "m16b")
        evac("v", 1, 0)
        evac("s", 1, 2)
        if t == 0:
            wait("v", "p4")
            sig(V.tensor_tensor_scan(T.p4[:, 8:12], T.p4[:, 0:4], T.p4[:, 4:8], 0.0, A.mult, A.add), "pg")
        evac("v", 1, 1)
        evac("s", 1, 3)
        if t == 0:
            wait("v", "qu")
            sig(V.tensor_copy(T.uq2[:].bitcast(dt.uint32), T.uq[:].bitcast(dt.uint32).indirect(T.uoff[:])), "upk")
            wait("s", "qu")
            sig(S.activation(T.up2[:], T.up[:].indirect(T.uoff[:]), F.Copy), "upk")
        qy_half(1)
        evac("s", 0, 0)
        evac("s", 0, 1)
        evac("s", 0, 3)
        evac("v", 0, 2)
        if t == 0:
            wait("s", "m16b")
            sig(S.activation(T.mk[:], T.m16b[:].indirect(T.o16[:]), F.Copy), "mk")
        qy_half(0)
        scores(1)
        scores(0)
        wait("g", "qy0", "qy1")
        g.remote_dma(u8(T["lq%d" % t][:]), u8(qy[:]), T.sem["aq%d" % t], T.sem.snt, pid, rid, mask)
        g.remote_dma(T["lp%d" % t][:], py[:], T.sem["aq%d" % t], T.sem.snt, pid, rid, mask)
        count["snt"] = count.get("snt", 0) + 2 * ne
        count["aq%d" % t] = 2 * ne
        if t == 0:
            wait("y", "qy0")
            sig(Y.dma_start(T.vin[:], T.v[:]), "lv", 16)
            wait("g", "etz")
            for b in range(4):
                sig(g.affine_select(T.et[:, 512 * b + b:512 * (b + 1):4], T.ones[:, 0:128], [[-1, 128]], A.is_equal, 0.0, 0, 1), "etc")
            sig(g.affine_select(T.keep4[:], T.ones[:, 0:C], [[0, C // 4], [1, 4]], A.not_equal, 0.0, 0, 0), "gu")
            wait("v", "cm")
        for h in (1, 0):
            wait("s", "pz%d" % h)
            sig(S.activation(T.zz[:, h * H:h * H + H], ps[4 * h + 1][:, 0:H], F.Copy), "z")

        def own(h):
            wait("v", "pv%d" % h)
            sig(V.tensor_tensor(T.mm[:, h * H:h * H + H], ps[4 * h][:, 0:H], T.cm[:], A.max), "m%d" % h)

        def held(h):
            wait("v", "m%d" % h)
            sig(V.tensor_tensor_scan(T.hh[:, h * H:h * H + H], T.cs[:], T.mm[:, h * H:h * H + H], 0.0, A.max, A.min), "h%d" % h)

        def inrun(h):
            wait("v", "h%d" % h)
            sig(V.tensor_tensor(T.ft[:, 4 * H * h + 3:4 * H * (h + 1):4], ps[4 * h][:, 0:H], T.hh[:, h * H:h * H + H], A.is_gt), "f0")

        def signs(q):
            for m in (NB - 1 - 2 * q, NB - 2 - 2 * q):
                lo, hi = (NB - 1 - m, m) if q < 4 else (CB, m if m == 15 else 16)
                sig(S.activation(T.sg[:, m - HB, 16 * lo:16 * hi], T.zz[:, 16 * lo:16 * hi], F.Sign, bias=T.hh[:, 16 * m + 15:16 * m + 16], scale=-1.0),
                    "sg%d" % q)

        def flags(q):
            wait("s", "sg%d" % q, "fz", "fz0")
            for k in range(2):
                m = NB - 1 - 2 * q - k
                lo = NB - 1 - m if q < 4 else CB
                i, a = T.sg[:, m - HB, 16 * lo:16 * m], FT[min(q, 3)] + 65 * k
                o = T.ft[:, a:a + 64 * (m - lo) - 3:4] if q < 4 else i
                sig(S.activation(o, i, F.Sign, bias=1.0, scale=-1.0, accum_out=T.cnt[:, m - HB:m - HB + 1]), "f%d" % q if q < 4 else "u1")
                if q > 3 and m < 15:
                    i = T.sg[:, m - HB, 16 * m + 16:256]
                    sig(S.activation(i, i, F.Relu, scale=-1.0, accum_out=T.cn2[:, m - CB:m - CB + 1]), "u1")

        def first(q):
            if q == 4:
                return [(m, FT[4] + 65 * (m - 7), 16 * (15 - m)) for m in range(7, CB)]
            return [(lo - 1, FT[q] + 64 * (lo - LO[q]) + 2 + (lo % 2 if q else 0), C - 32 * lo) for lo in (2 * q, 2 * q + 1) if lo]

        def rows(q):
            for m, a, w in first(q):
                sig(V.tensor_scalar(T.ft[:, a:a + 4 * w - 3:4], T.zz[:, 16 * m + 16:16 * m + 16 + w], T.hh[:, 16 * m + 15:16 * m + 16], None, A.is_gt),
                    "f%d" % q)

        def scans(q):
            for m, a, w in first(q):
                b = a + 4 * w - 3
                sig(V.tensor_tensor_scan(T.so[:, m, 176 - w // 2:176], T.ft[:, a:b:8], T.ft[:, a + 4:b:8], 0.0, A.add, A.add), "scn")

        def pack(q):
            wait("v", "f%d" % q)
            sig(V.quantize_mx(T.fq[:, QT[q]:QT[q] + TWD[q]], T.fp[:, QT[q]:QT[q] + TWD[q]], T.ft[:, FT[q]:FT[q + 1]]), "qf%d" % q)
            wait("p", "qf%d" % q)
            a, e = QT[q] - 16 * LO[q], QT[q] + TWD[q]
            ins = P.matmul_mx(ps[2][:, 0:e - a], T.bq[:], T.bp[:], T.fq[:, a:e], T.fp[:, a:e], q == 0, q == 3)
            if q == 3:
                sig(ins, "csm")

        own(1)
        held(1)
        if t == 0:
            wait("v", "fz")
        inrun(1)
        own(0)
        held(0)
        wait("s", "h1", "z")
        signs(0)
        for q in range(3):
            signs(q + 1)
            flags(q)
        flags(3)
        signs(4)
        wait("s", "h0")
        sig(S.activation(T.vb[:], T.zz[:, H:256], F.Sign, bias=T.hh[:, H - 1:H], scale=-1.0), "sg5")
        signs(5)
        flags(4)
        flags(5)
        sig(S.activation(T.vb[:], T.vb[:], F.Relu, scale=-1.0, accum_out=T.cn2[:, 0:1]), "u1")
        if t == 0:
            wait("v", "gb1")
            sig(V.quantize_mx(T.bq[:], T.bp[:], T.b1[:]), "qb")
        inrun(0)
        wait("v", "z")
        for q in range(4):
            rows(q)
        wait("p", "qb", "qz")
        pack(0)
        wait("v", "etz")
        rows(4)
        wait("p", "lz")
        pack(1)
        pack(4)
        scans(1)
        wait("v", "mk")
        sig(V.tensor_tensor_scan(T.st16[:], T.mk[:], T.ft[:, 3:4 * C:4], 0.0, A.mult, A.add), "st16")
        if t == 0:
            wait("v", "gj")
            sig(V.tensor_scalar(T.ni[:, 0:8], T.jj[:, 0:128:16], 2.0, 2.0 * MID + 16, A.mult, A.add), "st16")
            sig(V.tensor_scalar(T.ni[:, 8:CB], T.jj[:, 128:16 * CB:16], MID + 128.0, None, A.add), "st16")
            sig(V.memset(T.ni[:, CB:16], 16.0 * (8 + CB)), "st16")
            sig(V.tensor_scalar(T.ni[:, 16:NB], T.jj[:, 256:C:16], -2.0, 736.0 - 2 * MID, A.mult, A.add), "st16")
        pack(2)
        wait("v", "st16")
        sig(V.tensor_tensor(T.nv[:], T.st16[:, 15:C:16], T.ni[:], A.add), "scn")
        pack(3)
        for q in (2, 4, 3, 0):
            scans(q)
        if t == 0:
            wait("v", "etc")
            sig(V.quantize_mx(T.eq[:], T.ep[:], T.et[:]), "qe")
        wait("v", "scn")
        sig(V.tensor_tensor(T.uv[:], T.so[:, :, 175], T.nv[:], A.add), "u1")
        wait("v", "csm")
        sig(V.tensor_tensor_scan(T.xs[:], T.mk[:], ps[2][:, 0:C], 0.0, A.mult, A.add), "xs")
        wait("v", "u1")
        sig(V.tensor_tensor(T.uv[:, HB:NB], T.uv[:, HB:NB], T.cnt[:], A.add), "u2")
        wait("v", "xs")
        sig(V.tensor_scalar(T.u1[:], T.xs[:, 15:C:16], T.pg[:, 1:2], T.pg[:, 2:3], A.mult, A.subtract), "uu")
        wait("v", "u2")
        sig(V.tensor_tensor(T.uv[:, CB:15], T.uv[:, CB:15], T.cn2[:], A.add), "uu")
        wait("p", "qe", "aq%d" % t)
        for b in range(4):
            sig(P.matmul_mx(ps[4 + b][:, 0:C], T.eq[:, 128 * b:128 * b + 128], T.ep[:, 128 * b:128 * b + 128],
                            T["lq%d" % t][:], T["lp%d" % t][:], True, True), "r%d" % (4 + b))
        if t == 0:
            wait("s", "p4", "gj")
            for k in range(4):
                sig(S.activation(T.mask4[:, k:C:4], T.ones[:, 0:C // 4], F.Copy, scale=T.p4[:, 4 + k:5 + k]), "mask4")
            sig(S.activation(T.oo[:, C:C + K], T.jj[:, 0:K], F.Identity, bias=float(C)), "m4")
            wait("s", "mask4")
            sig(S.activation(T.m4[:], T.mask4[:, 0:K], F.Identity, bias=U4, scale=-U4 / 4), "m4")
        for b in range(4):
            wait("s", "r%d" % (4 + b))
            sig(S.activation(T.dd[:, b:4 * C:4], ps[4 + b][:, 0:C], F.Copy), "dE")
        wait("v", "uu")
        sig(V.tensor_tensor(T.ww[:], T.uv[:], T.u1[:], A.subtract), "ww")
        wait("v", "ww")
        sig(V.tensor_copy(T.off[:], T.ww[:]), "off")
        wait("v", "off")
        sig(V.tensor_copy(T.oo[:, 0:C].indirect(T.off[:]), T.jj[:]), "sct")
        if t == 0:
            wait("v", "m4", "pg", "gu")
        wait("v", "sct")
        sig(V.tensor_tensor_scan(T.bs[:], T.m4[:], T.oo[:, 0:K], 0.0, A.mult, A.add), "bs")
        wait("v", "bs")
        sig(V.tensor_scalar(T["lst%d" % t][:], T.bs[:, 3:K:4], T.p4[:, 11:12], tadd, A.mult, A.add), "lst")
        wait("g", "lst")
        g.remote_dma(T["ll%d" % t][:], T["lst%d" % t][:], T.sem["al%d" % t], T.sem.snt, pid, rid, mask)
        count["snt"] += ne
        count["al%d" % t] = ne
        sig(V.tensor_tensor(T.em[:], T.oo[:, K:C + K].indirect(T.off[:]), T.mask4[:], A.mult), "em")
        wait("v", "em")
        sig(V.tensor_tensor_scan(T.es[:], T.keep4[:], T.em[:], 0.0, A.mult, A.add), "es")
        wait("v", "es")
        sig(V.tensor_scalar(T.xoff[:], T.es[:, 3:C:4], tadd, None, A.add), "ext")
        if t == 0:
            wait("v", "lv")
            sig(V.quantize_mx(T.vq[:], T.vp[:], T.vin[:]), "qv")
        if t == R - 1:
            wait("s", "sct")
            sig(S.activation(T.olb[:], T.oo[:, 0:C], F.Identity, bias=float(MID)), "olb")
            wait("y", "olb")
            sig(Y.dma_start(T.ol[:], T.olb[0:128:16, :]), "st", 16)
        ll = T["ll%d" % t]
        wait("v", "dE", "al%d" % t)
        wait("s", "dE", "al%d" % t)
        sig(V.tensor_copy(yw[:, 4 * C:4 * C + 2 * K], T.dd[:].indirect(ll[:, 0:K // 8])), "ext")
        sig(S.activation(yw[:, 4 * C + 2 * K:4 * C + 4 * K], T.dd[:].indirect(ll[:, K // 8:K // 4]), F.Copy), "ext")

    state(R)
    qx, px = T["qx%d" % R], T["px%d" % R]
    wait("p", "qv")
    for h in (1, 0):
        wait("p", "qx%d" % h)
        sig(P.matmul_mx(ps[h][:, 0:H], T.vq[:], T.vp[:], qx[:, h * H:h * H + H], px[:, h * H:h * H + H], True, True), "ym%d" % h)
    wait("y", "qx1")
    sig(Y.dma_start(T.oc[:, 4 * H:4 * C], u8(qx[:, H:C])), "st", 16)
    wait("s", "ym1")
    sig(S.activation(T.yb[:, H:C], ps[1][:, 0:H], F.Copy), "yb1")
    wait("v", "ym0")
    sig(V.tensor_copy(T.yb[:, 0:H], ps[0][:, 0:H]), "yb0")
    wait("y", "yb1")
    sig(Y.dma_start(T.y[:, H:C], T.yb[:, H:C]), "st", 16)
    wait("y", "qx0")
    sig(Y.dma_start(T.oc[:, 0:4 * H], u8(qx[:, 0:H])), "st", 16)
    wait("s", "qx0", "qx1")
    for k in range(4):
        sig(S.dma_start(T.osc[4 * k:4 * k + 4, :], px[32 * k:32 * k + 4, :]), "st", 16)
    wait("y", "yb0")
    sig(Y.dma_start(T.y[:, 0:H], T.yb[:, 0:H]), "st", 16)
    for name in count:
        if max([v for (q, m), v in seen.items() if m == name] + [0]) < count[name]:
            wait("y", name)
